import numpy as np
import ml_dtypes


def mxq(x, axis, fmt="e4m3"):
    dtype, down = {"e4m3": (ml_dtypes.float8_e4m3fn, 7), "e5m2": (ml_dtypes.float8_e5m2, 14)}[fmt]
    v = np.moveaxis(np.asarray(x, np.float32).astype(ml_dtypes.bfloat16).astype(np.float64), axis, -1)
    blocks = v.reshape(v.shape[:-1] + (-1, 32))
    amax = np.abs(blocks).max(-1, keepdims=True)
    byte = np.maximum(np.where(amax > 0, np.frexp(amax)[1] - 1 + 127, 0) - down, 1)
    scale = np.exp2(byte - 127.0)
    codes = (blocks / scale).astype(np.float32).astype(dtype).astype(np.float64)
    return np.moveaxis((codes * scale).reshape(v.shape), -1, axis)


WIDE = False


def mx_kscale(k):
    if not WIDE:
        return np.ones(k)
    levels = np.array([30, -30])
    if k % 512:
        return np.exp2(np.random.permutation(np.resize(levels, k // 32))).repeat(32)
    a = np.empty((k // 512, 16))
    for p in range(k // 512):
        a[p, :8] = np.random.permutation(np.resize(levels, 8))
        for g in range(8):
            far = levels[np.abs(levels - a[p, g]) >= 10]
            a[p, g + 8] = far[np.random.randint(len(far))]
    return np.exp2(a.ravel()).repeat(32)


BF16 = ml_dtypes.bfloat16


def bf(x):
    return np.asarray(x, np.float32).astype(BF16)


def f64(x):
    return np.asarray(x).astype(np.float64)


E2M1 = np.array([0.0, 0.5, 1.0, 1.5, 2.0, 3.0, 4.0, 6.0, -0.0, -0.5, -1.0, -1.5, -2.0, -3.0, -4.0, -6.0])


def pack_weight(w, fmt):
    k, n = w.shape
    w = f64(bf(w)).reshape(k // 32, 32, n)
    amax = np.abs(w).max(1)
    if fmt == "e4m3":
        byte = np.frexp(amax)[1] - 1 + 127 - 7
    else:
        mant, ex = np.frexp(amax / 6.0)
        byte = np.where(mant > 0.5, ex, ex - 1) + 127
    byte = np.clip(np.where(amax > 0, byte, 1), 1, 254)
    scaled = (w * np.exp2(127.0 - byte)[:, None, :]).reshape(k, n).astype(np.float32)
    by_word = np.ascontiguousarray(scaled.reshape(k // 512, 128, 4, n).transpose(0, 1, 3, 2))
    if fmt == "e4m3":
        words = by_word.astype(ml_dtypes.float8_e4m3fn).view(np.uint8)
    else:
        c = by_word.astype(ml_dtypes.float4_e2m1fn).view(np.uint8) & 0xF
        words = c[..., 0::2] | (c[..., 1::2] << 4)
    return np.ascontiguousarray(words), np.ascontiguousarray(byte.astype(np.uint8).reshape(k // 512, 16, n))


def unpack_weight(words, scales, fmt):
    g, p, n, _ = words.shape
    if fmt == "e4m3":
        vals = np.ascontiguousarray(words).view(ml_dtypes.float8_e4m3fn).astype(np.float64)
    else:
        nib = np.empty((g, p, n, 4), np.uint8)
        nib[..., 0::2] = words & 0xF
        nib[..., 1::2] = words >> 4
        vals = E2M1[nib]
    vals = vals * np.repeat(np.exp2(scales.astype(np.float64) - 127.0), 8, axis=1)[..., None]
    return vals.transpose(0, 1, 3, 2).reshape(g * 512, n)
def pack4(w):
    words, scales = pack_weight(w, "e2m1")
    return words.reshape(words.shape[0], 128, -1), scales


def unpack4(words, scales):
    return unpack_weight(words.reshape(words.shape[0], 128, -1, 2), scales, "e2m1")


M, D, N = 1024, 1024, 2048

MATCH = 0.125
TEMP = 2.0


def setup_inputs():
    s, t = mx_kscale(D), mx_kscale(N)
    text = np.random.standard_normal((N, D)) / np.sqrt(D)
    y_words, y_scales = pack4(text.T / s[:, None] / t)
    sign = np.where(np.random.random((M, N)) < MATCH, -1.0, 1.0)
    temp = TEMP * (1 + 0.1 * np.random.standard_normal((M, N)))
    return {"x": bf(np.random.standard_normal((M, D)) * s),
            "y_words": y_words,
            "y_scales": y_scales,
            "b": bf((0.3 * np.random.standard_normal(N) - 0.5) / t),
            "c": bf(sign * temp * t),
            "v": bf(text / t[:, None])}


def reference(x, y_words, y_scales, b, c, v):
    sim = mxq(f64(x), 1, "e4m3") @ unpack4(y_words, y_scales)
    signed = f64(c)
    e = signed / (1 + np.exp(-signed * (sim + f64(b))))
    return mxq(e, 1, "e5m2") @ mxq(f64(v), 0, "e4m3")

@@ -1,0 +1,367 @@
+from contextlib import ExitStack
+
+import concourse.mybir as mybir
+from concourse.masks import make_identity
+
+M, D, N = 1024, 1024, 2048
+FLOPS = 2 * M * D * N * 2
+
+F32 = mybir.dt.float32
+BF16 = mybir.dt.bfloat16
+I32 = mybir.dt.int32
+U32 = mybir.dt.uint32
+U8 = mybir.dt.uint8
+E4M3X4 = mybir.dt.float8_e4m3fn_x4
+E5M2X4 = mybir.dt.float8_e5m2_x4
+E2M1X4 = mybir.dt.float4_e2m1fn_x4
+ALU = mybir.AluOpType
+ACT = mybir.ActivationFunctionType
+
+P = 128
+PACK = 4
+PASS = P * PACK
+BANK = 512
+TILES = BANK // P
+D_PASSES = D // PASS
+N_PASSES = N // PASS
+BLOCKS = M // BANK
+HALVES = D // BANK
+UNITS = BLOCKS * N_PASSES
+
+
+def tile_siglip_image_gradient_s9_kernel(tc, x, y_words, y_scales, b, c, v, out):
+    nc = tc.nc
+    with ExitStack() as ctx:
+        sb = ctx.enter_context(tc.tile_pool(name="sb", bufs=1))
+        ps = ctx.enter_context(tc.psum_pool(name="ps", bufs=1))
+        ctx.enter_context(tc.manual_schedule())
+
+        def bank(k, name):
+            return ps.tile([P, BANK], F32, name=name, tag="bank%d" % k)
+
+        def keep(shape, dtype, name):
+            return sb.tile(shape, dtype, name=name, tag=name, align_bytes=64)
+
+        def rotate(shape, dtype, name, tag, bufs):
+            return sb.tile(shape, dtype, name=name, tag=tag, bufs=bufs, align_bytes=64)
+
+        ys_raw = keep([P, D_PASSES, N], U8, "ys_raw")
+        nc.gpsimd.memset(ys_raw[:].rearrange("p h n -> p (h n)").bitcast(I32), 0)
+        warm = keep([P, 8], F32, "warm")
+        nc.gpsimd.memset(warm[:], 0.0)
+        nc.scalar.activation(out=warm[:, 1:2], in_=warm[:, 0:1], func=ACT.Sigmoid)
+        ident = keep([P, P], F32, "ident")
+        make_identity(nc, ident[:])
+
+        x_raw, y_raw, c_raw, v_raw = {}, {}, {}, {}
+        b_sb = keep([P, N_PASSES, PACK], BF16, "b_sb")
+
+        def load_x(blk, h):
+            x_raw[blk, h] = keep([P, TILES, PASS], BF16, "x_raw%d%d" % (blk, h))
+            src = x[blk * BANK:(blk + 1) * BANK, h * PASS:(h + 1) * PASS]
+            nc.sync.dma_start(out=x_raw[blk, h][:], in_=src.rearrange("(a p) k -> p a k", p=P))
+
+        def load_y(g):
+            y_raw[g] = keep([P, D_PASSES, 2 * PASS], U8, "y_raw%d" % g)
+            src = y_words[:, :, 2 * g * PASS:2 * (g + 1) * PASS].bitcast(I32)
+            nc.sync.dma_start(out=y_raw[g][:].bitcast(I32), in_=src.rearrange("h p w -> p h w"))
+
+        def load_y_scales():
+            for q in range(4):
+                src = y_scales[:, 4 * q:4 * q + 4, :].bitcast(I32)
+                nc.sync.dma_start(out=ys_raw[32 * q:32 * q + 4, :, :].bitcast(I32),
+                                  in_=src.rearrange("h r w -> r h w"))
+
+        def load_c(n):
+            blk, g = divmod(n, N_PASSES)
+            c_raw[n] = rotate([P, TILES, PASS], BF16, "c_raw%d" % n, "io", UNITS)
+            src = c[blk * BANK:(blk + 1) * BANK, g * PASS:(g + 1) * PASS]
+            nc.sync.dma_start(out=c_raw[n][:], in_=src.rearrange("(a p) j -> p a j", p=P))
+
+        def load_v(g, half):
+            v_raw[g, half] = keep([P, PACK, BANK], BF16, "v_raw%d%d" % (g, half))
+            src = v[g * PASS:(g + 1) * PASS, half * BANK:(half + 1) * BANK]
+            nc.sync.dma_start(out=v_raw[g, half][:], in_=src.rearrange("(p t) d -> p t d", t=PACK))
+
+        load_x(0, 0)
+        load_x(0, 1)
+        load_y(0)
+        load_y_scales()
+        load_c(0)
+        nc.sync.dma_start(out=b_sb[:], in_=b.rearrange("(g p t) -> p g t", p=P, t=PACK))
+        load_y(1)
+        load_c(1)
+        load_y(2)
+        load_c(2)
+        load_x(1, 0)
+        load_y(3)
+        load_c(3)
+        load_x(1, 1)
+        load_v(0, 0)
+        load_c(4)
+        load_v(1, 0)
+        load_c(5)
+        load_v(2, 0)
+        load_c(6)
+        load_c(7)
+        load_v(3, 0)
+        load_v(0, 1)
+        load_v(1, 1)
+        load_v(2, 1)
+        load_v(3, 1)
+
+        y_codes, y_planes = {}, {}
+
+        def sort_y(g):
+            y_codes[g] = keep([P, D_PASSES, PACK, P, 2], U8, "y_codes%d" % g)
+            nc.vector.tensor_copy(
+                out=y_codes[g][:],
+                in_=y_raw[g][:].rearrange("p h (m t e) -> p h t m e", t=PACK, e=2))
+            y_planes[g] = keep([P, D_PASSES, PACK, P], U8, "y_planes%d" % g)
+            nc.vector.tensor_copy(
+                out=y_planes[g][:],
+                in_=ys_raw[:, :, g * PASS:(g + 1) * PASS].rearrange("p h (m t) -> p h t m", t=PACK))
+
+        def turn(raw, banks, name):
+            words = raw[:].bitcast(F32)
+            turned = []
+            for pair in range(2):
+                bk = bank(banks[pair], "%s_%d" % (name, pair))
+                for a in range(2):
+                    for u in range(2):
+                        col = (2 * a + u) * P
+                        nc.tensor.transpose(bk[:, col:col + P], words[:, 2 * pair + a, u::2], ident[:])
+                turned.append(bk)
+            return turned
+
+        def gather_words(engine, dst, turned, pair):
+            dst_words = dst[:].bitcast(F32)[:, pair * BANK:(pair + 1) * BANK]
+            dst_words = dst_words.rearrange("p (a r u) -> p a r u", a=2, u=2)
+            src = turned[pair][:].rearrange("p (a u r) -> p a r u", a=2, u=2)
+            if engine == "s":
+                nc.scalar.copy(out=dst_words, in_=src)
+            else:
+                nc.vector.tensor_copy(out=dst_words, in_=src)
+
+        def quantize(src, fmt, name):
+            codes = keep([P, BANK], U32, name + "_codes")
+            plane = keep([P, BANK], U8, name + "_plane")
+            nc.vector.quantize_mx(out=codes[:].bitcast(fmt), scales=plane[:], in_=src[:])
+            return codes, plane
+
+        x_g, x_q, c_t, v_g, v_q, sim, z, sig, e_bf, e_q, acc = {}, {}, {}, {}, {}, {}, {}, {}, {}, {}, {}
+
+        def turn_x(blk, h, banks, engines):
+            turned = turn(x_raw[blk, h], banks, "xt%d%d" % (blk, h))
+            x_g[blk, h] = rotate([P, PACK * BANK], BF16, "x_g%d%d" % (blk, h), "grouped", 4)
+            for pair in range(2):
+                gather_words(engines[pair], x_g[blk, h], turned, pair)
+
+        def quant_x(blk, h):
+            x_q[blk, h] = quantize(x_g[blk, h], E4M3X4, "x%d%d" % (blk, h))
+
+        c_banks = {}
+
+        def turn_c(n, banks):
+            c_banks[n] = turn(c_raw[n], banks, "ct%d" % n)
+            c_t[n] = rotate([P, PACK * BANK], BF16, "c_t%d" % n, "c_t", 6)
+
+        def copy_c(n, pair, engine):
+            gather_words(engine, c_t[n], c_banks[n], pair)
+
+        def group_v(g, half, engine):
+            v_g[g, half] = rotate([P, PACK * BANK], BF16, "v_g%d%d" % (g, half), "grouped", 4)
+            dst = v_g[g, half][:].rearrange("p (d t) -> p d t", t=PACK)
+            src = v_raw[g, half][:].rearrange("p t d -> p d t")
+            if engine == "s":
+                nc.scalar.copy(out=dst, in_=src)
+            else:
+                nc.vector.tensor_copy(out=dst, in_=src)
+
+        def quant_v(g, half):
+            v_q[g, half] = quantize(v_g[g, half], E4M3X4, "v%d%d" % (g, half))
+
+        def similarities(n):
+            blk, g = divmod(n, N_PASSES)
+            for t in range(PACK):
+                sim[n, t] = bank(t, "sim%d_%d" % (n, t))
+                for h in range(D_PASSES):
+                    codes, plane = x_q[blk, h]
+                    nc.tensor.matmul_mx(
+                        out=sim[n, t][:],
+                        lhsT=y_codes[g][:, h, t, :, :].rearrange("p m e -> p (m e)").bitcast(E2M1X4),
+                        lhsT_scale=y_planes[g][:, h, t, :],
+                        rhs=codes[:].bitcast(E4M3X4), rhs_scale=plane[:],
+                        start=(h == 0), stop=(h == D_PASSES - 1))
+
+        def logits(n):
+            g = n % N_PASSES
+            c_slots = c_t[n][:].rearrange("p (i t) -> p t i", t=PACK)
+            for u in range(2):
+                z[n, u] = rotate([P, 2, BANK], F32, "z%d_%d" % (n, u), "z", 3)
+                for e in range(2):
+                    t = 2 * u + e
+                    nc.vector.scalar_tensor_tensor(
+                        out=z[n, u][:, e, :], in0=sim[n, t][:], scalar=b_sb[:, g, t:t + 1],
+                        in1=c_slots[:, t, :], op0=ALU.add, op1=ALU.mult)
+
+        def sigmoids(n):
+            sig[n] = rotate([P, 2, BANK, 2], F32, "sig%d" % n, "sig", 2)
+            for u in range(2):
+                nc.scalar.activation(out=sig[n][:, u, :, :], in_=z[n, u][:].rearrange("p e i -> p i e"),
+                                     func=ACT.Sigmoid)
+
+        def weigh(n, lo, hi, engine=nc.vector, fresh=True):
+            if lo == 0 and fresh:
+                e_bf[n] = rotate([P, PACK * BANK], BF16, "e_bf%d" % n, "e_bf", 1)
+            cols = slice(PACK * lo, PACK * hi)
+            engine.tensor_tensor(
+                out=e_bf[n][:, cols].rearrange("p (i u e) -> p i u e", u=2, e=2),
+                in0=sig[n][:, :, lo:hi, :].rearrange("p u i e -> p i u e"),
+                in1=c_t[n][:, cols].rearrange("p (i u e) -> p i u e", u=2, e=2),
+                op=ALU.mult)
+
+        def quant_e(n, lo, hi):
+            if lo == 0:
+                e_q[n] = (keep([P, BANK], U32, "e%d_codes" % n), keep([P, BANK], U8, "e%d_plane" % n))
+            codes, plane = e_q[n]
+            nc.vector.quantize_mx(out=codes[:, lo:hi].bitcast(E5M2X4), scales=plane[:, lo:hi],
+                                  in_=e_bf[n][:, PACK * lo:PACK * hi])
+
+        def gradient_pass(blk, a, half, g, k):
+            if g == 0:
+                acc[blk, a, half] = bank(k, "acc%d%d%d" % (blk, a, half))
+            e_codes, e_plane = e_q[blk * N_PASSES + g]
+            v_codes, v_plane = v_q[g, half]
+            nc.tensor.matmul_mx(
+                out=acc[blk, a, half][:],
+                lhsT=e_codes[:, a * P:(a + 1) * P].bitcast(E5M2X4), lhsT_scale=e_plane[:, a * P:(a + 1) * P],
+                rhs=v_codes[:].bitcast(E4M3X4), rhs_scale=v_plane[:],
+                start=(g == 0), stop=(g == N_PASSES - 1))
+
+        def sweep(blk, half, gs, first_bank):
+            for g in gs:
+                for a in range(TILES):
+                    gradient_pass(blk, a, half, g, first_bank + a)
+
+        def store(blk, a, half, engine):
+            res = rotate([P, BANK], F32, "res%d%d%d" % (blk, a, half), "io", UNITS)
+            if engine == "s":
+                nc.scalar.copy(out=res[:], in_=acc[blk, a, half][:])
+            else:
+                nc.vector.tensor_copy(out=res[:], in_=acc[blk, a, half][:])
+            row = blk * BANK + a * P
+            nc.sync.dma_start(out=out[row:row + P, half * BANK:(half + 1) * BANK], in_=res[:])
+
+        SH = 208
+
+        def begin(n):
+            if n > 0:
+                weigh(n - 1, 0, SH, nc.gpsimd)
+            logits(n)
+            if n + 1 < UNITS:
+                similarities(n + 1)
+
+        def both(n):
+            copy_c(n, 0, "s")
+            copy_c(n, 1, "s")
+
+        turn_x(0, 0, (4, 5), "sv")
+        turn_x(0, 1, (6, 7), "ss")
+        quant_x(0, 0)
+        sort_y(0)
+        turn_c(0, (4, 5))
+        quant_x(0, 1)
+        both(0)
+        similarities(0)
+        sort_y(1)
+        turn_c(1, (6, 7))
+        both(1)
+        begin(0)
+        sigmoids(0)
+        sort_y(2)
+        turn_c(2, (4, 5))
+        both(2)
+        turn_x(1, 0, (6, 7), "ss")
+        begin(1)
+        sigmoids(1)
+        weigh(0, SH, BANK)
+        sort_y(3)
+        quant_e(0, 0, BANK)
+        turn_c(3, (4, 5))
+        both(3)
+        turn_x(1, 1, (6, 7), "ss")
+        group_v(0, 0, "s")
+        begin(2)
+        sigmoids(2)
+        weigh(1, SH, BANK)
+        quant_x(1, 0)
+        quant_x(1, 1)
+        quant_v(0, 0)
+        quant_e(1, 0, BANK)
+        turn_c(4, (4, 5))
+        turn_c(5, (6, 7))
+        both(4)
+        group_v(1, 0, "s")
+        begin(3)
+        sigmoids(3)
+        both(5)
+        turn_c(6, (4, 5))
+        turn_c(7, (6, 7))
+        both(6)
+        both(7)
+        weigh(2, SH, BANK)
+        quant_v(1, 0)
+        group_v(2, 0, "v")
+        quant_e(2, 0, BANK)
+        begin(4)
+        sigmoids(4)
+        group_v(0, 1, "s")
+        weigh(3, SH, BANK)
+        quant_v(2, 0)
+        group_v(3, 0, "v")
+        quant_e(3, 0, BANK)
+        quant_v(3, 0)
+        group_v(1, 1, "s")
+        sweep(0, 0, (0, 1, 2, 3), 4)
+        begin(5)
+        for a in range(TILES):
+            store(0, a, 0, "s")
+        sigmoids(5)
+        quant_v(0, 1)
+        weigh(4, SH, BANK)
+        quant_v(1, 1)
+        group_v(2, 1, "v")
+        quant_e(4, 0, BANK)
+        quant_v(2, 1)
+        group_v(3, 1, "s")
+        sweep(0, 1, (0, 1, 2), 4)
+        begin(6)
+        sigmoids(6)
+        weigh(5, SH, BANK)
+        quant_v(3, 1)
+        quant_e(5, 0, BANK)
+        sweep(0, 1, (3,), 4)
+        for a in range(TILES):
+            store(0, a, 1, "s")
+        sweep(1, 0, (0, 1), 4)
+        begin(7)
+        sigmoids(7)
+        sweep(1, 1, (0, 1), 0)
+        weigh(6, SH, BANK)
+        quant_e(6, 0, 256)
+
+        e_bf[7] = keep([P, PACK * BANK], BF16, "e_last")
+        for a in range(TILES + 1):
+            if a < TILES:
+                weigh(7, a * P, (a + 1) * P, nc.vector, False)
+            if a == 0:
+                quant_e(6, 256, BANK)
+            if a > 0:
+                quant_e(7, (a - 1) * P, a * P)
+                for g in (2, 3):
+                    gradient_pass(1, a - 1, 0, g, 0)
+                    gradient_pass(1, a - 1, 1, g, 0)
+        for a in range(TILES):
+            store(1, a, 0, "s")
+            store(1, a, 1, "s" if a < 2 else "v")

@@ -27,6 +27,10 @@ N_PASSES = N // PASS
 BLOCKS = M // BANK
 HALVES = D // BANK
 UNITS = BLOCKS * N_PASSES
+CT_BUFS = 6
+Z_BUFS = 3
+SH = 208
+GS = 384
 
 
 def tile_siglip_image_gradient_s9_kernel(tc, x, y_words, y_scales, b, c, v, out):
@@ -46,23 +50,23 @@ def tile_siglip_image_gradient_s9_kernel(tc, x, y_words, y_scales, b, c, v, out)
             return sb.tile(shape, dtype, name=name, tag=tag, bufs=bufs, align_bytes=64)
 
         ys_raw = keep([P, D_PASSES, N], U8, "ys_raw")
-        nc.gpsimd.memset(ys_raw[:].rearrange("p h n -> p (h n)").bitcast(I32), 0)
+        nc.vector.memset(ys_raw[:].rearrange("p h n -> p (h n)").bitcast(I32), 0)
         warm = keep([P, 8], F32, "warm")
-        nc.gpsimd.memset(warm[:], 0.0)
-        nc.scalar.activation(out=warm[:, 1:2], in_=warm[:, 0:1], func=ACT.Sigmoid)
+        nc.vector.memset(warm[:], 0.0)
         ident = keep([P, P], F32, "ident")
         make_identity(nc, ident[:])
+        nc.scalar.activation(out=warm[:, 1:2], in_=warm[:, 0:1], func=ACT.Sigmoid)
 
         x_raw, y_raw, c_raw, v_raw = {}, {}, {}, {}
         b_sb = keep([P, N_PASSES, PACK], BF16, "b_sb")
 
-        def load_x(blk, h):
-            x_raw[blk, h] = keep([P, TILES, PASS], BF16, "x_raw%d%d" % (blk, h))
-            src = x[blk * BANK:(blk + 1) * BANK, h * PASS:(h + 1) * PASS]
-            nc.sync.dma_start(out=x_raw[blk, h][:], in_=src.rearrange("(a p) k -> p a k", p=P))
+        def load_x(blk, a):
+            x_raw[blk, a] = keep([P, D], BF16, "x_raw%d%d" % (blk, a))
+            row = blk * BANK + a * P
+            nc.sync.dma_start(out=x_raw[blk, a][:], in_=x[row:row + P, :])
 
         def load_y(g):
-            y_raw[g] = keep([P, D_PASSES, 2 * PASS], U8, "y_raw%d" % g)
+            y_raw[g] = rotate([P, D_PASSES, 2 * PASS], U8, "y_raw%d" % g, "vg" if g == N_PASSES - 1 else "y_raw%d" % g, 1)
             src = y_words[:, :, 2 * g * PASS:2 * (g + 1) * PASS].bitcast(I32)
             nc.sync.dma_start(out=y_raw[g][:].bitcast(I32), in_=src.rearrange("h p w -> p h w"))
 
@@ -83,153 +87,177 @@ def tile_siglip_image_gradient_s9_kernel(tc, x, y_words, y_scales, b, c, v, out)
             src = v[g * PASS:(g + 1) * PASS, half * BANK:(half + 1) * BANK]
             nc.sync.dma_start(out=v_raw[g, half][:], in_=src.rearrange("(p t) d -> p t d", t=PACK))
 
-        load_x(0, 0)
-        load_x(0, 1)
         load_y(0)
+        load_y(1)
+        for a in range(TILES):
+            load_x(0, a)
         load_y_scales()
         load_c(0)
         nc.sync.dma_start(out=b_sb[:], in_=b.rearrange("(g p t) -> p g t", p=P, t=PACK))
-        load_y(1)
-        load_c(1)
         load_y(2)
-        load_c(2)
-        load_x(1, 0)
+        load_c(1)
         load_y(3)
-        load_c(3)
-        load_x(1, 1)
         load_v(0, 0)
-        load_c(4)
+        load_c(2)
         load_v(1, 0)
-        load_c(5)
+        for a in range(TILES):
+            load_x(1, a)
+        load_c(3)
+        load_v(0, 1)
+        load_c(4)
         load_v(2, 0)
+        load_c(5)
+        load_v(3, 0)
         load_c(6)
         load_c(7)
-        load_v(3, 0)
-        load_v(0, 1)
         load_v(1, 1)
         load_v(2, 1)
         load_v(3, 1)
 
         y_codes, y_planes = {}, {}
 
-        def sort_y(g):
+        def sort_codes(g):
             y_codes[g] = keep([P, D_PASSES, PACK, P, 2], U8, "y_codes%d" % g)
             nc.vector.tensor_copy(
                 out=y_codes[g][:],
                 in_=y_raw[g][:].rearrange("p h (m t e) -> p h t m e", t=PACK, e=2))
+
+        def sort_planes(g):
             y_planes[g] = keep([P, D_PASSES, PACK, P], U8, "y_planes%d" % g)
             nc.vector.tensor_copy(
                 out=y_planes[g][:],
                 in_=ys_raw[:, :, g * PASS:(g + 1) * PASS].rearrange("p h (m t) -> p h t m", t=PACK))
 
-        def turn(raw, banks, name):
-            words = raw[:].bitcast(F32)
-            turned = []
-            for pair in range(2):
-                bk = bank(banks[pair], "%s_%d" % (name, pair))
-                for a in range(2):
-                    for u in range(2):
-                        col = (2 * a + u) * P
-                        nc.tensor.transpose(bk[:, col:col + P], words[:, 2 * pair + a, u::2], ident[:])
-                turned.append(bk)
-            return turned
-
-        def gather_words(engine, dst, turned, pair):
-            dst_words = dst[:].bitcast(F32)[:, pair * BANK:(pair + 1) * BANK]
-            dst_words = dst_words.rearrange("p (a r u) -> p a r u", a=2, u=2)
-            src = turned[pair][:].rearrange("p (a u r) -> p a r u", a=2, u=2)
-            if engine == "s":
-                nc.scalar.copy(out=dst_words, in_=src)
-            else:
-                nc.vector.tensor_copy(out=dst_words, in_=src)
-
-        def quantize(src, fmt, name):
-            codes = keep([P, BANK], U32, name + "_codes")
-            plane = keep([P, BANK], U8, name + "_plane")
-            nc.vector.quantize_mx(out=codes[:].bitcast(fmt), scales=plane[:], in_=src[:])
-            return codes, plane
-
-        x_g, x_q, c_t, v_g, v_q, sim, z, sig, e_bf, e_q, acc = {}, {}, {}, {}, {}, {}, {}, {}, {}, {}, {}
-
-        def turn_x(blk, h, banks, engines):
-            turned = turn(x_raw[blk, h], banks, "xt%d%d" % (blk, h))
-            x_g[blk, h] = rotate([P, PACK * BANK], BF16, "x_g%d%d" % (blk, h), "grouped", 4)
-            for pair in range(2):
-                gather_words(engines[pair], x_g[blk, h], turned, pair)
-
-        def quant_x(blk, h):
-            x_q[blk, h] = quantize(x_g[blk, h], E4M3X4, "x%d%d" % (blk, h))
-
-        c_banks = {}
-
-        def turn_c(n, banks):
-            c_banks[n] = turn(c_raw[n], banks, "ct%d" % n)
-            c_t[n] = rotate([P, PACK * BANK], BF16, "c_t%d" % n, "c_t", 6)
-
-        def copy_c(n, pair, engine):
-            gather_words(engine, c_t[n], c_banks[n], pair)
-
-        def group_v(g, half, engine):
-            v_g[g, half] = rotate([P, PACK * BANK], BF16, "v_g%d%d" % (g, half), "grouped", 4)
-            dst = v_g[g, half][:].rearrange("p (d t) -> p d t", t=PACK)
-            src = v_raw[g, half][:].rearrange("p t d -> p d t")
+        def copy_on(engine, dst, src):
             if engine == "s":
                 nc.scalar.copy(out=dst, in_=src)
             else:
                 nc.vector.tensor_copy(out=dst, in_=src)
 
+        def pair_words(engine, dst, bk):
+            copy_on(engine, dst.bitcast(F32).rearrange("p (a r u) -> p a r u", a=2, u=2),
+                    bk[:].rearrange("p (a u r) -> p a r u", a=2, u=2))
+
+        x_banks, x_g, x_q, c_banks, c_t, v_g, v_q = {}, {}, {}, {}, {}, {}, {}
+        sim, z, sig, e_bf, e_q, acc, passes = {}, {}, {}, {}, {}, {}, {}
+
+        def mx_tiles(name):
+            return keep([P, BANK], U32, name + "_codes"), keep([P, BANK], U8, name + "_plane")
+
+        def turn_x(blk, pair, banks):
+            for h in range(D_PASSES):
+                x_banks[blk, pair, h] = bank(banks[h], "xt%d%d%d" % (blk, pair, h))
+            for a in range(2):
+                words = x_raw[blk, 2 * pair + a][:].bitcast(F32)
+                for h in range(D_PASSES):
+                    for u in range(2):
+                        col = (2 * a + u) * P
+                        nc.tensor.transpose(x_banks[blk, pair, h][:, col:col + P],
+                                            words[:, 2 * P * h + u:2 * P * (h + 1):2], ident[:])
+
+        def copy_x(blk, pair, h, engine):
+            x_g[blk, pair, h] = rotate([P, 2 * PASS], BF16, "x_g%d%d%d" % (blk, pair, h), "x_g", 4)
+            pair_words(engine, x_g[blk, pair, h][:], x_banks[blk, pair, h])
+
+        def quant_x(blk, pair, h):
+            if pair == 0:
+                x_q[blk, h] = mx_tiles("x%d%d" % (blk, h))
+            codes, plane = x_q[blk, h]
+            cols = slice(pair * 2 * P, (pair + 1) * 2 * P)
+            nc.vector.quantize_mx(out=codes[:, cols].bitcast(E4M3X4), scales=plane[:, cols],
+                                  in_=x_g[blk, pair, h][:])
+
+        def turn_c(n, pair, k):
+            words = c_raw[n][:].bitcast(F32)
+            c_banks[n, pair] = bank(k, "ct%d_%d" % (n, pair))
+            for a in range(2):
+                for u in range(2):
+                    col = (2 * a + u) * P
+                    nc.tensor.transpose(c_banks[n, pair][:, col:col + P], words[:, 2 * pair + a, u::2], ident[:])
+
+        def copy_c(n, pair, engine):
+            if pair == 0:
+                c_t[n] = rotate([P, PACK * BANK], BF16, "c_t%d" % n, "c_t", CT_BUFS)
+            pair_words(engine, c_t[n][:, pair * 2 * PASS:(pair + 1) * 2 * PASS], c_banks[n, pair])
+
+        def group_v(g, half, lo, hi, engine, tag, bufs):
+            tile = rotate([P, PACK * (hi - lo)], BF16, "v_g%d%d_%d" % (g, half, lo), tag, bufs)
+            v_g.setdefault((g, half), []).append((lo, hi, tile))
+            dst = tile[:].rearrange("p (d t) -> p d t", t=PACK)
+            src = v_raw[g, half][:, :, lo:hi].rearrange("p t d -> p d t")
+            if engine == "g":
+                nc.gpsimd.tensor_scalar(out=dst, in0=src, scalar1=1.0, scalar2=0.0, op0=ALU.mult, op1=ALU.add)
+            else:
+                copy_on(engine, dst, src)
+
         def quant_v(g, half):
-            v_q[g, half] = quantize(v_g[g, half], E4M3X4, "v%d%d" % (g, half))
+            v_q[g, half] = mx_tiles("v%d%d" % (g, half))
+            codes, plane = v_q[g, half]
+            for lo, hi, tile in sorted(v_g[g, half], key=lambda part: -part[0]):
+                at = lo
+                while at < hi:
+                    width = max(w for w in (P, 2 * P, BANK) if at + w <= hi)
+                    nc.vector.quantize_mx(out=codes[:, at:at + width].bitcast(E4M3X4), scales=plane[:, at:at + width],
+                                          in_=tile[:, PACK * (at - lo):PACK * (at - lo + width)])
+                    at = at + width
+
+        def similarity_pass(n, t, h):
+            blk, g = divmod(n, N_PASSES)
+            if h == 0:
+                sim[n, t] = bank(t, "sim%d_%d" % (n, t))
+            codes, plane = x_q[blk, h]
+            nc.tensor.matmul_mx(
+                out=sim[n, t][:],
+                lhsT=y_codes[g][:, h, t, :, :].rearrange("p m e -> p (m e)").bitcast(E2M1X4),
+                lhsT_scale=y_planes[g][:, h, t, :],
+                rhs=codes[:].bitcast(E4M3X4), rhs_scale=plane[:],
+                start=(h == 0), stop=(h == D_PASSES - 1))
 
         def similarities(n):
-            blk, g = divmod(n, N_PASSES)
             for t in range(PACK):
-                sim[n, t] = bank(t, "sim%d_%d" % (n, t))
                 for h in range(D_PASSES):
-                    codes, plane = x_q[blk, h]
-                    nc.tensor.matmul_mx(
-                        out=sim[n, t][:],
-                        lhsT=y_codes[g][:, h, t, :, :].rearrange("p m e -> p (m e)").bitcast(E2M1X4),
-                        lhsT_scale=y_planes[g][:, h, t, :],
-                        rhs=codes[:].bitcast(E4M3X4), rhs_scale=plane[:],
-                        start=(h == 0), stop=(h == D_PASSES - 1))
+                    similarity_pass(n, t, h)
 
-        def logits(n):
+        def logits(n, lo=0, hi=BANK):
             g = n % N_PASSES
             c_slots = c_t[n][:].rearrange("p (i t) -> p t i", t=PACK)
             for u in range(2):
-                z[n, u] = rotate([P, 2, BANK], F32, "z%d_%d" % (n, u), "z", 3)
+                z[n, lo, u] = rotate([P, 2, hi - lo], F32, "z%d_%d_%d" % (n, lo, u), "z", Z_BUFS)
                 for e in range(2):
                     t = 2 * u + e
                     nc.vector.scalar_tensor_tensor(
-                        out=z[n, u][:, e, :], in0=sim[n, t][:], scalar=b_sb[:, g, t:t + 1],
-                        in1=c_slots[:, t, :], op0=ALU.add, op1=ALU.mult)
+                        out=z[n, lo, u][:, e, :], in0=sim[n, t][:, lo:hi], scalar=b_sb[:, g, t:t + 1],
+                        in1=c_slots[:, t, lo:hi], op0=ALU.add, op1=ALU.mult)
 
-        def sigmoids(n):
-            sig[n] = rotate([P, 2, BANK, 2], F32, "sig%d" % n, "sig", 2)
+        def sigmoids(n, lo=0, hi=BANK, tag="sig"):
+            tile = rotate([P, 2, hi - lo, 2], F32, "sig%d_%d" % (n, lo), tag, 2)
+            sig.setdefault(n, []).append((lo, hi, tile))
             for u in range(2):
-                nc.scalar.activation(out=sig[n][:, u, :, :], in_=z[n, u][:].rearrange("p e i -> p i e"),
+                nc.scalar.activation(out=tile[:, u, :, :], in_=z[n, lo, u][:].rearrange("p e i -> p i e"),
                                      func=ACT.Sigmoid)
 
-        def weigh(n, lo, hi, engine=nc.vector, fresh=True):
-            if lo == 0 and fresh:
-                e_bf[n] = rotate([P, PACK * BANK], BF16, "e_bf%d" % n, "e_bf", 1)
+        def new_e(n, tag="e_bf"):
+            e_bf[n] = rotate([P, PACK * BANK], BF16, "e_bf%d" % n, tag, 1)
+            e_q[n] = mx_tiles("e%d" % n)
+
+        def weigh(n, lo, hi, engine=nc.vector):
             cols = slice(PACK * lo, PACK * hi)
+            base, tile = [(s_lo, s) for s_lo, s_hi, s in sig[n] if s_lo <= lo and hi <= s_hi][0]
             engine.tensor_tensor(
                 out=e_bf[n][:, cols].rearrange("p (i u e) -> p i u e", u=2, e=2),
-                in0=sig[n][:, :, lo:hi, :].rearrange("p u i e -> p i u e"),
+                in0=tile[:, :, lo - base:hi - base, :].rearrange("p u i e -> p i u e"),
                 in1=c_t[n][:, cols].rearrange("p (i u e) -> p i u e", u=2, e=2),
                 op=ALU.mult)
 
-        def quant_e(n, lo, hi):
-            if lo == 0:
-                e_q[n] = (keep([P, BANK], U32, "e%d_codes" % n), keep([P, BANK], U8, "e%d_plane" % n))
+        def quant_e(n, lo=0, hi=BANK):
             codes, plane = e_q[n]
             nc.vector.quantize_mx(out=codes[:, lo:hi].bitcast(E5M2X4), scales=plane[:, lo:hi],
                                   in_=e_bf[n][:, PACK * lo:PACK * hi])
 
-        def gradient_pass(blk, a, half, g, k):
-            if g == 0:
+        def gradient_pass(blk, a, half, g, k=None):
+            done = passes.setdefault((blk, a, half), [])
+            done.append(g)
+            if len(done) == 1:
                 acc[blk, a, half] = bank(k, "acc%d%d%d" % (blk, a, half))
             e_codes, e_plane = e_q[blk * N_PASSES + g]
             v_codes, v_plane = v_q[g, half]
@@ -237,131 +265,184 @@ def tile_siglip_image_gradient_s9_kernel(tc, x, y_words, y_scales, b, c, v, out)
                 out=acc[blk, a, half][:],
                 lhsT=e_codes[:, a * P:(a + 1) * P].bitcast(E5M2X4), lhsT_scale=e_plane[:, a * P:(a + 1) * P],
                 rhs=v_codes[:].bitcast(E4M3X4), rhs_scale=v_plane[:],
-                start=(g == 0), stop=(g == N_PASSES - 1))
+                start=(len(done) == 1), stop=(len(done) == N_PASSES))
 
-        def sweep(blk, half, gs, first_bank):
+        def sweep(blk, groups, gs):
             for g in gs:
-                for a in range(TILES):
-                    gradient_pass(blk, a, half, g, first_bank + a)
+                for a, half, k in groups:
+                    gradient_pass(blk, a, half, g, k)
 
         def store(blk, a, half, engine):
             res = rotate([P, BANK], F32, "res%d%d%d" % (blk, a, half), "io", UNITS)
-            if engine == "s":
-                nc.scalar.copy(out=res[:], in_=acc[blk, a, half][:])
-            else:
-                nc.vector.tensor_copy(out=res[:], in_=acc[blk, a, half][:])
+            copy_on(engine, res[:], acc[blk, a, half][:])
             row = blk * BANK + a * P
             nc.sync.dma_start(out=out[row:row + P, half * BANK:(half + 1) * BANK], in_=res[:])
 
-        SH = 208
+        def turn_both(n, banks):
+            for pair in range(2):
+                turn_c(n, pair, banks[pair])
 
-        def begin(n):
-            if n > 0:
-                weigh(n - 1, 0, SH, nc.gpsimd)
-            logits(n)
-            if n + 1 < UNITS:
-                similarities(n + 1)
+        def copy_both(n, engines="ss"):
+            for pair in range(2):
+                copy_c(n, pair, engines[pair])
 
-        def both(n):
-            copy_c(n, 0, "s")
-            copy_c(n, 1, "s")
+        def both_c(n, banks):
+            turn_both(n, banks)
+            copy_both(n)
 
-        turn_x(0, 0, (4, 5), "sv")
-        turn_x(0, 1, (6, 7), "ss")
-        quant_x(0, 0)
-        sort_y(0)
-        turn_c(0, (4, 5))
-        quant_x(0, 1)
-        both(0)
+        def g_part(g, half):
+            group_v(g, half, 0, GS, "g", "vg", 1)
+
+        def s_part(g, half, engine="s"):
+            group_v(g, half, GS, BANK, engine, "vp", 2)
+
+        def s_whole(g, half):
+            group_v(g, half, 0, BANK, "s", "vs", 2)
+
+        sort_codes(0)
+        sort_codes(1)
+        turn_x(0, 0, (4, 5))
+        turn_x(0, 1, (6, 7))
+        copy_x(0, 0, 0, "s")
+        copy_x(0, 0, 1, "s")
+        copy_x(0, 1, 0, "s")
+        copy_x(0, 1, 1, "s")
+        quant_x(0, 0, 0)
+        quant_x(0, 0, 1)
+        sort_planes(0)
+        quant_x(0, 1, 0)
+        quant_x(0, 1, 1)
+        both_c(0, (4, 5))
         similarities(0)
-        sort_y(1)
-        turn_c(1, (6, 7))
-        both(1)
-        begin(0)
+        sort_planes(1)
+        sort_planes(2)
+        sort_codes(2)
+        both_c(1, (6, 7))
+        logits(0)
+        similarities(1)
         sigmoids(0)
-        sort_y(2)
-        turn_c(2, (4, 5))
-        both(2)
-        turn_x(1, 0, (6, 7), "ss")
-        begin(1)
+        sort_planes(3)
+        sort_codes(3)
+        s_part(0, 0)
+        both_c(2, (4, 5))
+        g_part(0, 0)
+        logits(1)
+        turn_x(1, 0, (6, 7))
+        similarities(2)
         sigmoids(1)
-        weigh(0, SH, BANK)
-        sort_y(3)
-        quant_e(0, 0, BANK)
-        turn_c(3, (4, 5))
-        both(3)
-        turn_x(1, 1, (6, 7), "ss")
-        group_v(0, 0, "s")
-        begin(2)
-        sigmoids(2)
-        weigh(1, SH, BANK)
-        quant_x(1, 0)
-        quant_x(1, 1)
+        new_e(0)
+        weigh(0, 0, BANK)
         quant_v(0, 0)
-        quant_e(1, 0, BANK)
-        turn_c(4, (4, 5))
-        turn_c(5, (6, 7))
-        both(4)
-        group_v(1, 0, "s")
-        begin(3)
-        sigmoids(3)
-        both(5)
-        turn_c(6, (4, 5))
-        turn_c(7, (6, 7))
-        both(6)
-        both(7)
-        weigh(2, SH, BANK)
+        quant_e(0)
+        copy_x(1, 0, 0, "s")
+        copy_x(1, 0, 1, "s")
+        turn_x(1, 1, (4, 5))
+        s_part(1, 0)
+        copy_x(1, 1, 0, "s")
+        copy_x(1, 1, 1, "s")
+        turn_both(3, (6, 7))
+        g_part(1, 0)
+        logits(2)
+        similarities(3)
+        copy_both(3)
+        sigmoids(2)
+        new_e(1)
+        weigh(1, 0, BANK)
+        quant_x(1, 0, 0)
+        quant_x(1, 0, 1)
+        quant_x(1, 1, 0)
+        quant_x(1, 1, 1)
         quant_v(1, 0)
-        group_v(2, 0, "v")
-        quant_e(2, 0, BANK)
-        begin(4)
-        sigmoids(4)
-        group_v(0, 1, "s")
-        weigh(3, SH, BANK)
+        quant_e(1)
+        first = [(0, 0, 4), (1, 0, 5)]
+        second = [(2, 0, 6), (3, 0, 7)]
+        both_c(4, (4, 5))
+        both_c(5, (6, 7))
+        s_part(2, 0)
+        g_part(2, 0)
+        logits(3)
+        turn_both(6, (4, 5))
+        similarities(4)
+        copy_both(6)
+        sigmoids(3)
+        new_e(2)
+        weigh(2, 0, BANK)
         quant_v(2, 0)
-        group_v(3, 0, "v")
-        quant_e(3, 0, BANK)
+        quant_e(2)
+        both_c(7, (6, 7))
+        s_part(3, 0)
+        s_whole(0, 1)
+        sweep(0, first + second, (0, 1))
+        g_part(3, 0)
+        logits(4)
+        similarities(5)
+        sweep(0, first + second, (2,))
+        sigmoids(4)
+        new_e(3)
+        weigh(3, 0, BANK)
         quant_v(3, 0)
-        group_v(1, 1, "s")
-        sweep(0, 0, (0, 1, 2, 3), 4)
-        begin(5)
+        quant_e(3)
+        quant_v(0, 1)
+        sweep(0, first + second, (3,))
+        s_whole(1, 1)
+        g_part(2, 1)
+        logits(5)
         for a in range(TILES):
             store(0, a, 0, "s")
+        upper = [(a, 1, 4 + a) for a in range(TILES)]
+        similarities(6)
+        sweep(0, upper, (0,))
+        s_part(2, 1)
         sigmoids(5)
-        quant_v(0, 1)
-        weigh(4, SH, BANK)
+        s_part(3, 1)
+        new_e(4)
         quant_v(1, 1)
-        group_v(2, 1, "v")
-        quant_e(4, 0, BANK)
+        weigh(4, 0, BANK)
         quant_v(2, 1)
-        group_v(3, 1, "s")
-        sweep(0, 1, (0, 1, 2), 4)
-        begin(6)
-        sigmoids(6)
-        weigh(5, SH, BANK)
+        quant_e(4)
+        sweep(0, upper, (1, 2))
+        g_part(3, 1)
+        logits(6)
+        early = [(0, 0, 4), (0, 1, 5), (1, 0, 6), (1, 1, 7)]
+        late = [(2, 0, 0), (2, 1, 1), (3, 0, 2), (3, 1, 3)]
         quant_v(3, 1)
-        quant_e(5, 0, BANK)
-        sweep(0, 1, (3,), 4)
+        similarities(7)
+        sweep(0, upper, (3,))
+        sigmoids(6)
+        new_e(5)
+        weigh(5, 0, 256)
+        weigh(5, 256, BANK)
         for a in range(TILES):
             store(0, a, 1, "s")
-        sweep(1, 0, (0, 1), 4)
-        begin(7)
-        sigmoids(7)
-        sweep(1, 1, (0, 1), 0)
-        weigh(6, SH, BANK)
-        quant_e(6, 0, 256)
+        sweep(1, early, (0,))
+        quant_e(5, 0, 256)
+        quant_e(5, 256, BANK)
+        sweep(1, early, (1,))
 
-        e_bf[7] = keep([P, PACK * BANK], BF16, "e_last")
-        for a in range(TILES + 1):
-            if a < TILES:
-                weigh(7, a * P, (a + 1) * P, nc.vector, False)
-            if a == 0:
-                quant_e(6, 256, BANK)
-            if a > 0:
-                quant_e(7, (a - 1) * P, a * P)
-                for g in (2, 3):
-                    gradient_pass(1, a - 1, 0, g, 0)
-                    gradient_pass(1, a - 1, 1, g, 0)
+        new_e(6)
+        new_e(7, "e_last")
+        weigh(6, 0, SH, nc.gpsimd)
+        logits(7, 0, 256)
+        sigmoids(7, 0, 256)
+        logits(7, 256, BANK)
+        sigmoids(7, 256, BANK, "vs")
+        sweep(1, late, (0, 1))
+        weigh(6, SH, 256)
+        weigh(7, 0, P)
+        quant_e(6, 0, 256)
+        weigh(7, P, 2 * P)
+        quant_e(7, 0, P)
+        quant_e(7, P, 2 * P)
+        sweep(1, early[:2], (2, 3))
+        sweep(1, early[2:], (2, 3))
+        weigh(6, 256, BANK)
+        weigh(7, 2 * P, 3 * P)
+        quant_e(6, 256, BANK)
+        weigh(7, 3 * P, 4 * P)
+        quant_e(7, 2 * P, 3 * P)
+        quant_e(7, 3 * P, 4 * P)
+        sweep(1, late[:2], (2, 3))
+        sweep(1, late[2:], (2, 3))
         for a in range(TILES):
             store(1, a, 0, "s")
             store(1, a, 1, "s" if a < 2 else "v")

@@ -21,16 +21,20 @@ P = 128
 PACK = 4
 PASS = P * PACK
 BANK = 512
+PAIR = 2 * P
 TILES = BANK // P
 D_PASSES = D // PASS
 N_PASSES = N // PASS
-BLOCKS = M // BANK
-HALVES = D // BANK
-UNITS = BLOCKS * N_PASSES
-CT_BUFS = 6
-Z_BUFS = 3
-SH = 208
-GS = 384
+UNITS = (M // BANK) * N_PASSES
+
+GPSIMD_V_COLUMNS = 384
+GPSIMD_E_IMAGES = 208
+
+SIM_BANKS = (0, 1, 2, 3)
+LOW_BANKS, HIGH_BANKS = (4, 5), (6, 7)
+
+C_BUFS = 6
+LOGIT_BUFS = 3
 
 
 def tile_siglip_image_gradient_s9_kernel(tc, x, y_words, y_scales, b, c, v, out):
@@ -49,8 +53,13 @@ def tile_siglip_image_gradient_s9_kernel(tc, x, y_words, y_scales, b, c, v, out)
         def rotate(shape, dtype, name, tag, bufs):
             return sb.tile(shape, dtype, name=name, tag=tag, bufs=bufs, align_bytes=64)
 
-        ys_raw = keep([P, D_PASSES, N], U8, "ys_raw")
-        nc.vector.memset(ys_raw[:].rearrange("p h n -> p (h n)").bitcast(I32), 0)
+        def mx_tiles(name):
+            return keep([P, BANK], U32, name + "_codes"), keep([P, BANK], U8, name + "_plane")
+
+        ys_raw = {}
+        for lo, hi in ((0, PASS), (PASS, N)):
+            ys_raw[lo] = keep([P, D_PASSES, hi - lo], U8, "ys_raw%d" % lo)
+            nc.vector.memset(ys_raw[lo][:].rearrange("p h n -> p (h n)").bitcast(I32), 0)
         warm = keep([P, 8], F32, "warm")
         nc.vector.memset(warm[:], 0.0)
         ident = keep([P, P], F32, "ident")
@@ -60,20 +69,21 @@ def tile_siglip_image_gradient_s9_kernel(tc, x, y_words, y_scales, b, c, v, out)
         x_raw, y_raw, c_raw, v_raw = {}, {}, {}, {}
         b_sb = keep([P, N_PASSES, PACK], BF16, "b_sb")
 
-        def load_x(blk, a):
-            x_raw[blk, a] = keep([P, D], BF16, "x_raw%d%d" % (blk, a))
-            row = blk * BANK + a * P
-            nc.sync.dma_start(out=x_raw[blk, a][:], in_=x[row:row + P, :])
+        def load_x(blk):
+            for a in range(TILES):
+                x_raw[blk, a] = keep([P, D], BF16, "x_raw%d%d" % (blk, a))
+                row = blk * BANK + a * P
+                nc.sync.dma_start(out=x_raw[blk, a][:], in_=x[row:row + P, :])
 
-        def load_y(g):
-            y_raw[g] = rotate([P, D_PASSES, 2 * PASS], U8, "y_raw%d" % g, "vg" if g == N_PASSES - 1 else "y_raw%d" % g, 1)
+        def load_y(g, tag):
+            y_raw[g] = rotate([P, D_PASSES, 2 * PASS], U8, "y_raw%d" % g, tag, 1)
             src = y_words[:, :, 2 * g * PASS:2 * (g + 1) * PASS].bitcast(I32)
             nc.sync.dma_start(out=y_raw[g][:].bitcast(I32), in_=src.rearrange("h p w -> p h w"))
 
-        def load_y_scales():
+        def load_y_scales(lo, hi):
             for q in range(4):
-                src = y_scales[:, 4 * q:4 * q + 4, :].bitcast(I32)
-                nc.sync.dma_start(out=ys_raw[32 * q:32 * q + 4, :, :].bitcast(I32),
+                src = y_scales[:, 4 * q:4 * q + 4, lo:hi].bitcast(I32)
+                nc.sync.dma_start(out=ys_raw[lo][32 * q:32 * q + 4, :, :].bitcast(I32),
                                   in_=src.rearrange("h r w -> r h w"))
 
         def load_c(n):
@@ -87,31 +97,30 @@ def tile_siglip_image_gradient_s9_kernel(tc, x, y_words, y_scales, b, c, v, out)
             src = v[g * PASS:(g + 1) * PASS, half * BANK:(half + 1) * BANK]
             nc.sync.dma_start(out=v_raw[g, half][:], in_=src.rearrange("(p t) d -> p t d", t=PACK))
 
-        load_y(0)
-        load_y(1)
-        for a in range(TILES):
-            load_x(0, a)
-        load_y_scales()
+        load_y(0, "y_raw0")
+        load_y(1, "y_raw1")
+        load_x(0)
+        load_y_scales(0, PASS)
         load_c(0)
         nc.sync.dma_start(out=b_sb[:], in_=b.rearrange("(g p t) -> p g t", p=P, t=PACK))
-        load_y(2)
-        load_c(1)
-        load_y(3)
+        load_y_scales(PASS, N)
+        load_y(2, "v_gpsimd")
         load_v(0, 0)
-        load_c(2)
-        load_v(1, 0)
-        for a in range(TILES):
-            load_x(1, a)
-        load_c(3)
         load_v(0, 1)
-        load_c(4)
+        load_c(1)
+        load_y(3, "y_raw3")
+        load_v(1, 0)
+        load_c(2)
+        load_x(1)
         load_v(2, 0)
-        load_c(5)
+        load_c(3)
+        load_c(4)
         load_v(3, 0)
+        load_c(5)
         load_c(6)
-        load_c(7)
-        load_v(1, 1)
         load_v(2, 1)
+        load_v(1, 1)
+        load_c(7)
         load_v(3, 1)
 
         y_codes, y_planes = {}, {}
@@ -122,27 +131,21 @@ def tile_siglip_image_gradient_s9_kernel(tc, x, y_words, y_scales, b, c, v, out)
                 out=y_codes[g][:],
                 in_=y_raw[g][:].rearrange("p h (m t e) -> p h t m e", t=PACK, e=2))
 
-        def sort_planes(g):
+        def sort_plane(g):
+            staged = ys_raw[0][:] if g == 0 else ys_raw[PASS][:, :, (g - 1) * PASS:g * PASS]
             y_planes[g] = keep([P, D_PASSES, PACK, P], U8, "y_planes%d" % g)
-            nc.vector.tensor_copy(
-                out=y_planes[g][:],
-                in_=ys_raw[:, :, g * PASS:(g + 1) * PASS].rearrange("p h (m t) -> p h t m", t=PACK))
+            nc.vector.tensor_copy(out=y_planes[g][:], in_=staged.rearrange("p h (m t) -> p h t m", t=PACK))
 
-        def copy_on(engine, dst, src):
-            if engine == "s":
-                nc.scalar.copy(out=dst, in_=src)
-            else:
-                nc.vector.tensor_copy(out=dst, in_=src)
+        def turn(bk, a, words):
+            for u in range(2):
+                col = (2 * a + u) * P
+                nc.tensor.transpose(bk[:, col:col + P], words[:, u::2], ident[:])
 
-        def pair_words(engine, dst, bk):
-            copy_on(engine, dst.bitcast(F32).rearrange("p (a r u) -> p a r u", a=2, u=2),
-                    bk[:].rearrange("p (a u r) -> p a r u", a=2, u=2))
+        def join_words(dst, bk):
+            nc.scalar.copy(out=dst.bitcast(F32).rearrange("p (a r u) -> p a r u", a=2, u=2),
+                           in_=bk[:].rearrange("p (a u r) -> p a r u", a=2, u=2))
 
-        x_banks, x_g, x_q, c_banks, c_t, v_g, v_q = {}, {}, {}, {}, {}, {}, {}
-        sim, z, sig, e_bf, e_q, acc, passes = {}, {}, {}, {}, {}, {}, {}
-
-        def mx_tiles(name):
-            return keep([P, BANK], U32, name + "_codes"), keep([P, BANK], U8, name + "_plane")
+        x_banks, x_joined, x_mx = {}, {}, {}
 
         def turn_x(blk, pair, banks):
             for h in range(D_PASSES):
@@ -150,97 +153,75 @@ def tile_siglip_image_gradient_s9_kernel(tc, x, y_words, y_scales, b, c, v, out)
             for a in range(2):
                 words = x_raw[blk, 2 * pair + a][:].bitcast(F32)
                 for h in range(D_PASSES):
-                    for u in range(2):
-                        col = (2 * a + u) * P
-                        nc.tensor.transpose(x_banks[blk, pair, h][:, col:col + P],
-                                            words[:, 2 * P * h + u:2 * P * (h + 1):2], ident[:])
+                    turn(x_banks[blk, pair, h], a, words[:, h * PAIR:(h + 1) * PAIR])
 
-        def copy_x(blk, pair, h, engine):
-            x_g[blk, pair, h] = rotate([P, 2 * PASS], BF16, "x_g%d%d%d" % (blk, pair, h), "x_g", 4)
-            pair_words(engine, x_g[blk, pair, h][:], x_banks[blk, pair, h])
+        def copy_x(blk, pair):
+            for h in range(D_PASSES):
+                x_joined[blk, pair, h] = rotate([P, PACK * PAIR], BF16, "x_joined%d%d%d" % (blk, pair, h),
+                                                "x_joined", 2 * D_PASSES)
+                join_words(x_joined[blk, pair, h][:], x_banks[blk, pair, h])
 
-        def quant_x(blk, pair, h):
-            if pair == 0:
-                x_q[blk, h] = mx_tiles("x%d%d" % (blk, h))
-            codes, plane = x_q[blk, h]
-            cols = slice(pair * 2 * P, (pair + 1) * 2 * P)
-            nc.vector.quantize_mx(out=codes[:, cols].bitcast(E4M3X4), scales=plane[:, cols],
-                                  in_=x_g[blk, pair, h][:])
+        def quantize_x(blk, pair):
+            for h in range(D_PASSES):
+                if pair == 0:
+                    x_mx[blk, h] = mx_tiles("x%d%d" % (blk, h))
+                codes, plane = x_mx[blk, h]
+                cols = slice(pair * PAIR, (pair + 1) * PAIR)
+                nc.vector.quantize_mx(out=codes[:, cols].bitcast(E4M3X4), scales=plane[:, cols],
+                                      in_=x_joined[blk, pair, h][:])
 
-        def turn_c(n, pair, k):
-            words = c_raw[n][:].bitcast(F32)
-            c_banks[n, pair] = bank(k, "ct%d_%d" % (n, pair))
-            for a in range(2):
-                for u in range(2):
-                    col = (2 * a + u) * P
-                    nc.tensor.transpose(c_banks[n, pair][:, col:col + P], words[:, 2 * pair + a, u::2], ident[:])
+        sim = {}
 
-        def copy_c(n, pair, engine):
-            if pair == 0:
-                c_t[n] = rotate([P, PACK * BANK], BF16, "c_t%d" % n, "c_t", CT_BUFS)
-            pair_words(engine, c_t[n][:, pair * 2 * PASS:(pair + 1) * 2 * PASS], c_banks[n, pair])
-
-        def group_v(g, half, lo, hi, engine, tag, bufs):
-            tile = rotate([P, PACK * (hi - lo)], BF16, "v_g%d%d_%d" % (g, half, lo), tag, bufs)
-            v_g.setdefault((g, half), []).append((lo, hi, tile))
-            dst = tile[:].rearrange("p (d t) -> p d t", t=PACK)
-            src = v_raw[g, half][:, :, lo:hi].rearrange("p t d -> p d t")
-            if engine == "g":
-                nc.gpsimd.tensor_scalar(out=dst, in0=src, scalar1=1.0, scalar2=0.0, op0=ALU.mult, op1=ALU.add)
-            else:
-                copy_on(engine, dst, src)
-
-        def quant_v(g, half):
-            v_q[g, half] = mx_tiles("v%d%d" % (g, half))
-            codes, plane = v_q[g, half]
-            for lo, hi, tile in sorted(v_g[g, half], key=lambda part: -part[0]):
-                at = lo
-                while at < hi:
-                    width = max(w for w in (P, 2 * P, BANK) if at + w <= hi)
-                    nc.vector.quantize_mx(out=codes[:, at:at + width].bitcast(E4M3X4), scales=plane[:, at:at + width],
-                                          in_=tile[:, PACK * (at - lo):PACK * (at - lo + width)])
-                    at = at + width
-
-        def similarity_pass(n, t, h):
+        def similarities(n, slots=range(PACK)):
             blk, g = divmod(n, N_PASSES)
-            if h == 0:
-                sim[n, t] = bank(t, "sim%d_%d" % (n, t))
-            codes, plane = x_q[blk, h]
-            nc.tensor.matmul_mx(
-                out=sim[n, t][:],
-                lhsT=y_codes[g][:, h, t, :, :].rearrange("p m e -> p (m e)").bitcast(E2M1X4),
-                lhsT_scale=y_planes[g][:, h, t, :],
-                rhs=codes[:].bitcast(E4M3X4), rhs_scale=plane[:],
-                start=(h == 0), stop=(h == D_PASSES - 1))
-
-        def similarities(n):
-            for t in range(PACK):
+            for t in slots:
+                sim[n, t] = bank(SIM_BANKS[t], "sim%d_%d" % (n, t))
                 for h in range(D_PASSES):
-                    similarity_pass(n, t, h)
+                    codes, plane = x_mx[blk, h]
+                    nc.tensor.matmul_mx(
+                        out=sim[n, t][:],
+                        lhsT=y_codes[g][:, h, t, :, :].rearrange("p m e -> p (m e)").bitcast(E2M1X4),
+                        lhsT_scale=y_planes[g][:, h, t, :],
+                        rhs=codes[:].bitcast(E4M3X4), rhs_scale=plane[:],
+                        start=(h == 0), stop=(h == D_PASSES - 1))
+
+        c_banks, c_t, logit, sig, e_bf, e_mx = {}, {}, {}, {}, {}, {}
+
+        def turn_c(n, banks):
+            words = c_raw[n][:].bitcast(F32)
+            for pair in range(2):
+                c_banks[n, pair] = bank(banks[pair], "ct%d_%d" % (n, pair))
+                for a in range(2):
+                    turn(c_banks[n, pair], a, words[:, 2 * pair + a, :])
+
+        def copy_c(n):
+            c_t[n] = rotate([P, PACK * BANK], BF16, "c_t%d" % n, "c_t", C_BUFS)
+            for pair in range(2):
+                join_words(c_t[n][:, pair * PACK * PAIR:(pair + 1) * PACK * PAIR], c_banks[n, pair])
 
         def logits(n, lo=0, hi=BANK):
             g = n % N_PASSES
             c_slots = c_t[n][:].rearrange("p (i t) -> p t i", t=PACK)
             for u in range(2):
-                z[n, lo, u] = rotate([P, 2, hi - lo], F32, "z%d_%d_%d" % (n, lo, u), "z", Z_BUFS)
+                logit[n, lo, u] = rotate([P, 2, hi - lo], F32, "logit%d_%d_%d" % (n, lo, u), "logit", LOGIT_BUFS)
                 for e in range(2):
                     t = 2 * u + e
                     nc.vector.scalar_tensor_tensor(
-                        out=z[n, lo, u][:, e, :], in0=sim[n, t][:, lo:hi], scalar=b_sb[:, g, t:t + 1],
+                        out=logit[n, lo, u][:, e, :], in0=sim[n, t][:, lo:hi], scalar=b_sb[:, g, t:t + 1],
                         in1=c_slots[:, t, lo:hi], op0=ALU.add, op1=ALU.mult)
 
         def sigmoids(n, lo=0, hi=BANK, tag="sig"):
             tile = rotate([P, 2, hi - lo, 2], F32, "sig%d_%d" % (n, lo), tag, 2)
             sig.setdefault(n, []).append((lo, hi, tile))
             for u in range(2):
-                nc.scalar.activation(out=tile[:, u, :, :], in_=z[n, lo, u][:].rearrange("p e i -> p i e"),
+                nc.scalar.activation(out=tile[:, u, :, :], in_=logit[n, lo, u][:].rearrange("p e i -> p i e"),
                                      func=ACT.Sigmoid)
 
         def new_e(n, tag="e_bf"):
             e_bf[n] = rotate([P, PACK * BANK], BF16, "e_bf%d" % n, tag, 1)
-            e_q[n] = mx_tiles("e%d" % n)
+            e_mx[n] = mx_tiles("e%d" % n)
 
-        def weigh(n, lo, hi, engine=nc.vector):
+        def make_e(n, lo, hi, engine=nc.vector):
             cols = slice(PACK * lo, PACK * hi)
             base, tile = [(s_lo, s) for s_lo, s_hi, s in sig[n] if s_lo <= lo and hi <= s_hi][0]
             engine.tensor_tensor(
@@ -249,200 +230,217 @@ def tile_siglip_image_gradient_s9_kernel(tc, x, y_words, y_scales, b, c, v, out)
                 in1=c_t[n][:, cols].rearrange("p (i u e) -> p i u e", u=2, e=2),
                 op=ALU.mult)
 
-        def quant_e(n, lo=0, hi=BANK):
-            codes, plane = e_q[n]
+        def quantize_e(n, lo=0, hi=BANK):
+            codes, plane = e_mx[n]
             nc.vector.quantize_mx(out=codes[:, lo:hi].bitcast(E5M2X4), scales=plane[:, lo:hi],
                                   in_=e_bf[n][:, PACK * lo:PACK * hi])
 
-        def gradient_pass(blk, a, half, g, k=None):
-            done = passes.setdefault((blk, a, half), [])
-            done.append(g)
-            if len(done) == 1:
-                acc[blk, a, half] = bank(k, "acc%d%d%d" % (blk, a, half))
-            e_codes, e_plane = e_q[blk * N_PASSES + g]
-            v_codes, v_plane = v_q[g, half]
-            nc.tensor.matmul_mx(
-                out=acc[blk, a, half][:],
-                lhsT=e_codes[:, a * P:(a + 1) * P].bitcast(E5M2X4), lhsT_scale=e_plane[:, a * P:(a + 1) * P],
-                rhs=v_codes[:].bitcast(E4M3X4), rhs_scale=v_plane[:],
-                start=(len(done) == 1), stop=(len(done) == N_PASSES))
+        v_parts, v_mx = {}, {}
 
-        def sweep(blk, groups, gs):
+        def v_part(g, half, lo, hi, tag, bufs):
+            tile = rotate([P, PACK * (hi - lo)], BF16, "v_part%d%d_%d" % (g, half, lo), tag, bufs)
+            v_parts.setdefault((g, half), []).append((lo, hi, tile))
+            return tile[:], v_raw[g, half][:, :, lo:hi]
+
+        def interleave_v_scalar(g, half, lo, tag):
+            dst, src = v_part(g, half, lo, BANK, tag, 2)
+            nc.scalar.copy(out=dst.rearrange("p (d i t) -> p d t i", i=4, t=PACK),
+                           in_=src.rearrange("p t (d i) -> p d t i", i=4))
+
+        def v_whole_scalar(g, half):
+            interleave_v_scalar(g, half, 0, "v_whole")
+
+        def v_rest_scalar(g, half):
+            interleave_v_scalar(g, half, GPSIMD_V_COLUMNS, "v_rest")
+
+        def v_share_gpsimd(g, half):
+            dst, src = v_part(g, half, 0, GPSIMD_V_COLUMNS, "v_gpsimd", 1)
+            nc.gpsimd.tensor_scalar(out=dst.rearrange("p (d t) -> p d t", t=PACK), in0=src.rearrange("p t d -> p d t"),
+                                    scalar1=1.0, scalar2=0.0, op0=ALU.mult, op1=ALU.add)
+
+        def quantize_v(g, half):
+            v_mx[g, half] = mx_tiles("v%d%d" % (g, half))
+            codes, plane = v_mx[g, half]
+            for lo, hi, tile in v_parts[g, half]:
+                at = lo
+                while at < hi:
+                    width = max(w for w in (P, PAIR, BANK) if at + w <= hi)
+                    nc.vector.quantize_mx(out=codes[:, at:at + width].bitcast(E4M3X4), scales=plane[:, at:at + width],
+                                          in_=tile[:, PACK * (at - lo):PACK * (at - lo + width)])
+                    at = at + width
+
+        acc, passes_done = {}, {}
+
+        def add_passes(blk, sums, gs):
             for g in gs:
-                for a, half, k in groups:
-                    gradient_pass(blk, a, half, g, k)
+                for a, half, k in sums:
+                    done = passes_done.setdefault((blk, a, half), [])
+                    done.append(g)
+                    if len(done) == 1:
+                        acc[blk, a, half] = bank(k, "acc%d%d%d" % (blk, a, half))
+                    e_codes, e_plane = e_mx[blk * N_PASSES + g]
+                    v_codes, v_plane = v_mx[g, half]
+                    nc.tensor.matmul_mx(
+                        out=acc[blk, a, half][:],
+                        lhsT=e_codes[:, a * P:(a + 1) * P].bitcast(E5M2X4), lhsT_scale=e_plane[:, a * P:(a + 1) * P],
+                        rhs=v_codes[:].bitcast(E4M3X4), rhs_scale=v_plane[:],
+                        start=(len(done) == 1), stop=(len(done) == N_PASSES))
 
-        def store(blk, a, half, engine):
+        def store(blk, a, half, copy=nc.scalar.copy):
             res = rotate([P, BANK], F32, "res%d%d%d" % (blk, a, half), "io", UNITS)
-            copy_on(engine, res[:], acc[blk, a, half][:])
+            copy(out=res[:], in_=acc[blk, a, half][:])
             row = blk * BANK + a * P
             nc.sync.dma_start(out=out[row:row + P, half * BANK:(half + 1) * BANK], in_=res[:])
 
-        def turn_both(n, banks):
-            for pair in range(2):
-                turn_c(n, pair, banks[pair])
-
-        def copy_both(n, engines="ss"):
-            for pair in range(2):
-                copy_c(n, pair, engines[pair])
-
-        def both_c(n, banks):
-            turn_both(n, banks)
-            copy_both(n)
-
-        def g_part(g, half):
-            group_v(g, half, 0, GS, "g", "vg", 1)
-
-        def s_part(g, half, engine="s"):
-            group_v(g, half, GS, BANK, engine, "vp", 2)
-
-        def s_whole(g, half):
-            group_v(g, half, 0, BANK, "s", "vs", 2)
+        free_banks = LOW_BANKS + HIGH_BANKS
+        left_sums = [(a, 0, free_banks[a]) for a in range(TILES)]
+        right_sums = [(a, 1, free_banks[a]) for a in range(TILES)]
+        last_banks = free_banks + SIM_BANKS
+        tile_sums = [[(a, half, last_banks[2 * a + half]) for half in range(2)] for a in range(TILES)]
 
         sort_codes(0)
         sort_codes(1)
-        turn_x(0, 0, (4, 5))
-        turn_x(0, 1, (6, 7))
-        copy_x(0, 0, 0, "s")
-        copy_x(0, 0, 1, "s")
-        copy_x(0, 1, 0, "s")
-        copy_x(0, 1, 1, "s")
-        quant_x(0, 0, 0)
-        quant_x(0, 0, 1)
-        sort_planes(0)
-        quant_x(0, 1, 0)
-        quant_x(0, 1, 1)
-        both_c(0, (4, 5))
+        turn_x(0, 0, LOW_BANKS)
+        turn_x(0, 1, HIGH_BANKS)
+        copy_x(0, 0)
+        copy_x(0, 1)
+        quantize_x(0, 0)
+        sort_plane(0)
+        quantize_x(0, 1)
+        turn_c(0, LOW_BANKS)
+        copy_c(0)
         similarities(0)
-        sort_planes(1)
-        sort_planes(2)
+        sort_plane(1)
         sort_codes(2)
-        both_c(1, (6, 7))
+        v_rest_scalar(0, 0)
+        v_whole_scalar(0, 1)
+        turn_c(1, HIGH_BANKS)
+        copy_c(1)
+
+        v_share_gpsimd(0, 0)
         logits(0)
         similarities(1)
         sigmoids(0)
-        sort_planes(3)
+        sort_plane(2)
+        sort_plane(3)
         sort_codes(3)
-        s_part(0, 0)
-        both_c(2, (4, 5))
-        g_part(0, 0)
+        quantize_v(0, 0)
+        v_rest_scalar(1, 0)
+        turn_c(2, LOW_BANKS)
+        copy_c(2)
+
+        v_share_gpsimd(1, 0)
         logits(1)
-        turn_x(1, 0, (6, 7))
+        turn_x(1, 0, HIGH_BANKS)
         similarities(2)
         sigmoids(1)
         new_e(0)
-        weigh(0, 0, BANK)
-        quant_v(0, 0)
-        quant_e(0)
-        copy_x(1, 0, 0, "s")
-        copy_x(1, 0, 1, "s")
-        turn_x(1, 1, (4, 5))
-        s_part(1, 0)
-        copy_x(1, 1, 0, "s")
-        copy_x(1, 1, 1, "s")
-        turn_both(3, (6, 7))
-        g_part(1, 0)
+        make_e(0, 0, BANK)
+        quantize_v(1, 0)
+        quantize_e(0)
+        copy_x(1, 0)
+        turn_x(1, 1, LOW_BANKS)
+        v_rest_scalar(2, 0)
+        copy_x(1, 1)
+        turn_c(3, HIGH_BANKS)
+
+        v_share_gpsimd(2, 0)
         logits(2)
-        similarities(3)
-        copy_both(3)
+        similarities(3, (0, 1))
+        turn_c(4, LOW_BANKS)
+        similarities(3, (2, 3))
+        copy_c(3)
         sigmoids(2)
         new_e(1)
-        weigh(1, 0, BANK)
-        quant_x(1, 0, 0)
-        quant_x(1, 0, 1)
-        quant_x(1, 1, 0)
-        quant_x(1, 1, 1)
-        quant_v(1, 0)
-        quant_e(1)
-        first = [(0, 0, 4), (1, 0, 5)]
-        second = [(2, 0, 6), (3, 0, 7)]
-        both_c(4, (4, 5))
-        both_c(5, (6, 7))
-        s_part(2, 0)
-        g_part(2, 0)
+        make_e(1, 0, BANK)
+        quantize_x(1, 0)
+        quantize_x(1, 1)
+        quantize_v(2, 0)
+        quantize_e(1)
+        copy_c(4)
+        turn_c(5, HIGH_BANKS)
+        copy_c(5)
+        v_rest_scalar(3, 0)
+
+        v_share_gpsimd(3, 0)
         logits(3)
-        turn_both(6, (4, 5))
+        turn_c(6, LOW_BANKS)
         similarities(4)
-        copy_both(6)
+        copy_c(6)
         sigmoids(3)
         new_e(2)
-        weigh(2, 0, BANK)
-        quant_v(2, 0)
-        quant_e(2)
-        both_c(7, (6, 7))
-        s_part(3, 0)
-        s_whole(0, 1)
-        sweep(0, first + second, (0, 1))
-        g_part(3, 0)
+        make_e(2, 0, BANK)
+        quantize_v(3, 0)
+        quantize_e(2)
+        turn_c(7, HIGH_BANKS)
+        v_rest_scalar(2, 1)
+        copy_c(7)
+        v_whole_scalar(1, 1)
+        add_passes(0, left_sums, (0, 1))
+
+        v_share_gpsimd(2, 1)
         logits(4)
         similarities(5)
-        sweep(0, first + second, (2,))
+        add_passes(0, left_sums, (2,))
         sigmoids(4)
         new_e(3)
-        weigh(3, 0, BANK)
-        quant_v(3, 0)
-        quant_e(3)
-        quant_v(0, 1)
-        sweep(0, first + second, (3,))
-        s_whole(1, 1)
-        g_part(2, 1)
+        make_e(3, 0, BANK)
+        quantize_v(0, 1)
+        quantize_e(3)
+        quantize_v(2, 1)
+        add_passes(0, left_sums, (3,))
+        v_rest_scalar(3, 1)
+
+        v_share_gpsimd(3, 1)
         logits(5)
         for a in range(TILES):
-            store(0, a, 0, "s")
-        upper = [(a, 1, 4 + a) for a in range(TILES)]
+            store(0, a, 0)
         similarities(6)
-        sweep(0, upper, (0,))
-        s_part(2, 1)
+        quantize_v(1, 1)
+        quantize_v(3, 1)
+        for one_sum in right_sums:
+            add_passes(0, [one_sum], (0, 2, 1, 3))
         sigmoids(5)
-        s_part(3, 1)
+        for a in range(2):
+            store(0, a, 1)
         new_e(4)
-        quant_v(1, 1)
-        weigh(4, 0, BANK)
-        quant_v(2, 1)
-        quant_e(4)
-        sweep(0, upper, (1, 2))
-        g_part(3, 1)
-        logits(6)
-        early = [(0, 0, 4), (0, 1, 5), (1, 0, 6), (1, 1, 7)]
-        late = [(2, 0, 0), (2, 1, 1), (3, 0, 2), (3, 1, 3)]
-        quant_v(3, 1)
-        similarities(7)
-        sweep(0, upper, (3,))
-        sigmoids(6)
+        make_e(4, 0, PAIR)
+        make_e(4, PAIR, BANK)
+        quantize_e(4, 0, PAIR)
+        quantize_e(4, PAIR, BANK)
+
         new_e(5)
-        weigh(5, 0, 256)
-        weigh(5, 256, BANK)
-        for a in range(TILES):
-            store(0, a, 1, "s")
-        sweep(1, early, (0,))
-        quant_e(5, 0, 256)
-        quant_e(5, 256, BANK)
-        sweep(1, early, (1,))
+        make_e(5, 0, GPSIMD_E_IMAGES, nc.gpsimd)
+        logits(6)
+        similarities(7)
+        sigmoids(6)
+        for a in range(2, TILES):
+            store(0, a, 1)
+        make_e(5, GPSIMD_E_IMAGES, PAIR)
+        make_e(5, PAIR, BANK)
+        quantize_e(5, 0, PAIR)
+        quantize_e(5, PAIR, BANK)
+        for a in range(2):
+            add_passes(1, tile_sums[a], (0, 1))
 
         new_e(6)
         new_e(7, "e_last")
-        weigh(6, 0, SH, nc.gpsimd)
-        logits(7, 0, 256)
-        sigmoids(7, 0, 256)
-        logits(7, 256, BANK)
-        sigmoids(7, 256, BANK, "vs")
-        sweep(1, late, (0, 1))
-        weigh(6, SH, 256)
-        weigh(7, 0, P)
-        quant_e(6, 0, 256)
-        weigh(7, P, 2 * P)
-        quant_e(7, 0, P)
-        quant_e(7, P, 2 * P)
-        sweep(1, early[:2], (2, 3))
-        sweep(1, early[2:], (2, 3))
-        weigh(6, 256, BANK)
-        weigh(7, 2 * P, 3 * P)
-        quant_e(6, 256, BANK)
-        weigh(7, 3 * P, 4 * P)
-        quant_e(7, 2 * P, 3 * P)
-        quant_e(7, 3 * P, 4 * P)
-        sweep(1, late[:2], (2, 3))
-        sweep(1, late[2:], (2, 3))
+        make_e(6, 0, GPSIMD_E_IMAGES, nc.gpsimd)
+        logits(7, 0, PAIR)
+        sigmoids(7, 0, PAIR)
+        logits(7, PAIR, BANK)
+        sigmoids(7, PAIR, BANK, "v_whole")
+        add_passes(1, tile_sums[2] + tile_sums[3], (0, 1))
+        for pair, first_image in ((0, GPSIMD_E_IMAGES), (1, PAIR)):
+            lo, mid, hi = pair * PAIR, pair * PAIR + P, (pair + 1) * PAIR
+            make_e(6, first_image, hi)
+            make_e(7, lo, mid)
+            quantize_e(6, lo, hi)
+            make_e(7, mid, hi)
+            quantize_e(7, lo, mid)
+            quantize_e(7, mid, hi)
+            for a in (2 * pair, 2 * pair + 1):
+                add_passes(1, tile_sums[a], (2, 3))
         for a in range(TILES):
-            store(1, a, 0, "s")
-            store(1, a, 1, "s" if a < 2 else "v")
+            store(1, a, 0)
+            store(1, a, 1, nc.scalar.copy if a < 2 else nc.vector.tensor_copy)

@@ -56,10 +56,8 @@ def tile_siglip_image_gradient_s9_kernel(tc, x, y_words, y_scales, b, c, v, out)
         def mx_tiles(name):
             return keep([P, BANK], U32, name + "_codes"), keep([P, BANK], U8, name + "_plane")
 
-        ys_raw = {}
-        for lo, hi in ((0, PASS), (PASS, N)):
-            ys_raw[lo] = keep([P, D_PASSES, hi - lo], U8, "ys_raw%d" % lo)
-            nc.vector.memset(ys_raw[lo][:].rearrange("p h n -> p (h n)").bitcast(I32), 0)
+        ys_raw = keep([P, D_PASSES, N], U8, "ys_raw")
+        nc.vector.memset(ys_raw[:].rearrange("p h n -> p (h n)").bitcast(I32), 0)
         warm = keep([P, 8], F32, "warm")
         nc.vector.memset(warm[:], 0.0)
         ident = keep([P, P], F32, "ident")
@@ -69,8 +67,8 @@ def tile_siglip_image_gradient_s9_kernel(tc, x, y_words, y_scales, b, c, v, out)
         x_raw, y_raw, c_raw, v_raw = {}, {}, {}, {}
         b_sb = keep([P, N_PASSES, PACK], BF16, "b_sb")
 
-        def load_x(blk):
-            for a in range(TILES):
+        def load_x(blk, pair):
+            for a in (2 * pair, 2 * pair + 1):
                 x_raw[blk, a] = keep([P, D], BF16, "x_raw%d%d" % (blk, a))
                 row = blk * BANK + a * P
                 nc.sync.dma_start(out=x_raw[blk, a][:], in_=x[row:row + P, :])
@@ -80,10 +78,10 @@ def tile_siglip_image_gradient_s9_kernel(tc, x, y_words, y_scales, b, c, v, out)
             src = y_words[:, :, 2 * g * PASS:2 * (g + 1) * PASS].bitcast(I32)
             nc.sync.dma_start(out=y_raw[g][:].bitcast(I32), in_=src.rearrange("h p w -> p h w"))
 
-        def load_y_scales(lo, hi):
+        def load_y_scales():
             for q in range(4):
-                src = y_scales[:, 4 * q:4 * q + 4, lo:hi].bitcast(I32)
-                nc.sync.dma_start(out=ys_raw[lo][32 * q:32 * q + 4, :, :].bitcast(I32),
+                src = y_scales[:, 4 * q:4 * q + 4, :].bitcast(I32)
+                nc.sync.dma_start(out=ys_raw[32 * q:32 * q + 4, :, :].bitcast(I32),
                                   in_=src.rearrange("h r w -> r h w"))
 
         def load_c(n):
@@ -98,30 +96,31 @@ def tile_siglip_image_gradient_s9_kernel(tc, x, y_words, y_scales, b, c, v, out)
             nc.sync.dma_start(out=v_raw[g, half][:], in_=src.rearrange("(p t) d -> p t d", t=PACK))
 
         load_y(0, "y_raw0")
-        load_y(1, "y_raw1")
-        load_x(0)
-        load_y_scales(0, PASS)
+        load_x(0, 0)
+        load_y_scales()
+        load_x(0, 1)
         load_c(0)
         nc.sync.dma_start(out=b_sb[:], in_=b.rearrange("(g p t) -> p g t", p=P, t=PACK))
-        load_y_scales(PASS, N)
+        load_y(1, "y_raw1")
         load_y(2, "v_gpsimd")
         load_v(0, 0)
-        load_v(0, 1)
         load_c(1)
         load_y(3, "y_raw3")
         load_v(1, 0)
         load_c(2)
-        load_x(1)
+        load_x(1, 0)
+        load_x(1, 1)
         load_v(2, 0)
         load_c(3)
         load_c(4)
         load_v(3, 0)
         load_c(5)
         load_c(6)
-        load_v(2, 1)
-        load_v(1, 1)
         load_c(7)
+        load_v(2, 1)
+        load_v(0, 1)
         load_v(3, 1)
+        load_v(1, 1)
 
         y_codes, y_planes = {}, {}
 
@@ -132,7 +131,7 @@ def tile_siglip_image_gradient_s9_kernel(tc, x, y_words, y_scales, b, c, v, out)
                 in_=y_raw[g][:].rearrange("p h (m t e) -> p h t m e", t=PACK, e=2))
 
         def sort_plane(g):
-            staged = ys_raw[0][:] if g == 0 else ys_raw[PASS][:, :, (g - 1) * PASS:g * PASS]
+            staged = ys_raw[:, :, g * PASS:(g + 1) * PASS]
             y_planes[g] = keep([P, D_PASSES, PACK, P], U8, "y_planes%d" % g)
             nc.vector.tensor_copy(out=y_planes[g][:], in_=staged.rearrange("p h (m t) -> p h t m", t=PACK))
 
@@ -298,22 +297,23 @@ def tile_siglip_image_gradient_s9_kernel(tc, x, y_words, y_scales, b, c, v, out)
         last_banks = free_banks + SIM_BANKS
         tile_sums = [[(a, half, last_banks[2 * a + half]) for half in range(2)] for a in range(TILES)]
 
-        sort_codes(0)
-        sort_codes(1)
         turn_x(0, 0, LOW_BANKS)
         turn_x(0, 1, HIGH_BANKS)
         copy_x(0, 0)
         copy_x(0, 1)
-        quantize_x(0, 0)
+        sort_codes(0)
         sort_plane(0)
+        sort_plane(1)
+        quantize_x(0, 0)
+        sort_plane(2)
+        sort_plane(3)
         quantize_x(0, 1)
         turn_c(0, LOW_BANKS)
         copy_c(0)
         similarities(0)
-        sort_plane(1)
+        sort_codes(1)
         sort_codes(2)
         v_rest_scalar(0, 0)
-        v_whole_scalar(0, 1)
         turn_c(1, HIGH_BANKS)
         copy_c(1)
 
@@ -321,8 +321,6 @@ def tile_siglip_image_gradient_s9_kernel(tc, x, y_words, y_scales, b, c, v, out)
         logits(0)
         similarities(1)
         sigmoids(0)
-        sort_plane(2)
-        sort_plane(3)
         sort_codes(3)
         quantize_v(0, 0)
         v_rest_scalar(1, 0)
@@ -375,7 +373,7 @@ def tile_siglip_image_gradient_s9_kernel(tc, x, y_words, y_scales, b, c, v, out)
         turn_c(7, HIGH_BANKS)
         v_rest_scalar(2, 1)
         copy_c(7)
-        v_whole_scalar(1, 1)
+        v_whole_scalar(0, 1)
         add_passes(0, left_sums, (0, 1))
 
         v_share_gpsimd(2, 1)
@@ -390,16 +388,17 @@ def tile_siglip_image_gradient_s9_kernel(tc, x, y_words, y_scales, b, c, v, out)
         quantize_v(2, 1)
         add_passes(0, left_sums, (3,))
         v_rest_scalar(3, 1)
+        v_whole_scalar(1, 1)
 
         v_share_gpsimd(3, 1)
         logits(5)
         for a in range(TILES):
             store(0, a, 0)
         similarities(6)
-        quantize_v(1, 1)
         quantize_v(3, 1)
+        quantize_v(1, 1)
         for one_sum in right_sums:
-            add_passes(0, [one_sum], (0, 2, 1, 3))
+            add_passes(0, [one_sum], (0, 2, 3, 1))
         sigmoids(5)
         for a in range(2):
             store(0, a, 1)

from contextlib import ExitStack

import concourse.mybir as mybir
from concourse.masks import make_identity

M, D, N = 1024, 1024, 2048
FLOPS = 2 * M * D * N * 2

F32 = mybir.dt.float32
BF16 = mybir.dt.bfloat16
I32 = mybir.dt.int32
U32 = mybir.dt.uint32
U8 = mybir.dt.uint8
E4M3X4 = mybir.dt.float8_e4m3fn_x4
E5M2X4 = mybir.dt.float8_e5m2_x4
E2M1X4 = mybir.dt.float4_e2m1fn_x4
ALU = mybir.AluOpType
ACT = mybir.ActivationFunctionType

P = 128
PACK = 4
PASS = P * PACK
BANK = 512
PAIR = 2 * P
TILES = BANK // P
D_PASSES = D // PASS
N_PASSES = N // PASS
UNITS = (M // BANK) * N_PASSES

GPSIMD_V_COLUMNS = 384
GPSIMD_E_IMAGES = 208

SIM_BANKS = (0, 1, 2, 3)
LOW_BANKS, HIGH_BANKS = (4, 5), (6, 7)

C_BUFS = 6
LOGIT_BUFS = 3


def tile_siglip_image_gradient_s9_kernel(tc, x, y_words, y_scales, b, c, v, out):
    nc = tc.nc
    with ExitStack() as ctx:
        sb = ctx.enter_context(tc.tile_pool(name="sb", bufs=1))
        ps = ctx.enter_context(tc.psum_pool(name="ps", bufs=1))
        ctx.enter_context(tc.manual_schedule())

        def bank(k, name):
            return ps.tile([P, BANK], F32, name=name, tag="bank%d" % k)

        def keep(shape, dtype, name):
            return sb.tile(shape, dtype, name=name, tag=name, align_bytes=64)

        def rotate(shape, dtype, name, tag, bufs):
            return sb.tile(shape, dtype, name=name, tag=tag, bufs=bufs, align_bytes=64)

        def mx_tiles(name):
            return keep([P, BANK], U32, name + "_codes"), keep([P, BANK], U8, name + "_plane")

        ys_raw = keep([P, D_PASSES, N], U8, "ys_raw")
        nc.vector.memset(ys_raw[:].rearrange("p h n -> p (h n)").bitcast(I32), 0)
        warm = keep([P, 8], F32, "warm")
        nc.vector.memset(warm[:], 0.0)
        ident = keep([P, P], F32, "ident")
        make_identity(nc, ident[:])
        nc.scalar.activation(out=warm[:, 1:2], in_=warm[:, 0:1], func=ACT.Sigmoid)

        x_raw, y_raw, c_raw, v_raw = {}, {}, {}, {}
        b_sb = keep([P, N_PASSES, PACK], BF16, "b_sb")

        def load_x(blk, pair):
            for a in (2 * pair, 2 * pair + 1):
                x_raw[blk, a] = keep([P, D], BF16, "x_raw%d%d" % (blk, a))
                row = blk * BANK + a * P
                nc.sync.dma_start(out=x_raw[blk, a][:], in_=x[row:row + P, :])

        def load_y(g, tag):
            y_raw[g] = rotate([P, D_PASSES, 2 * PASS], U8, "y_raw%d" % g, tag, 1)
            src = y_words[:, :, 2 * g * PASS:2 * (g + 1) * PASS].bitcast(I32)
            nc.sync.dma_start(out=y_raw[g][:].bitcast(I32), in_=src.rearrange("h p w -> p h w"))

        def load_y_scales():
            for q in range(4):
                src = y_scales[:, 4 * q:4 * q + 4, :].bitcast(I32)
                nc.sync.dma_start(out=ys_raw[32 * q:32 * q + 4, :, :].bitcast(I32),
                                  in_=src.rearrange("h r w -> r h w"))

        def load_c(n):
            blk, g = divmod(n, N_PASSES)
            c_raw[n] = rotate([P, TILES, PASS], BF16, "c_raw%d" % n, "io", UNITS)
            src = c[blk * BANK:(blk + 1) * BANK, g * PASS:(g + 1) * PASS]
            nc.sync.dma_start(out=c_raw[n][:], in_=src.rearrange("(a p) j -> p a j", p=P))

        def load_v(g, half):
            v_raw[g, half] = keep([P, PACK, BANK], BF16, "v_raw%d%d" % (g, half))
            src = v[g * PASS:(g + 1) * PASS, half * BANK:(half + 1) * BANK]
            nc.sync.dma_start(out=v_raw[g, half][:], in_=src.rearrange("(p t) d -> p t d", t=PACK))

        load_y(0, "y_raw0")
        load_x(0, 0)
        load_y_scales()
        load_x(0, 1)
        load_c(0)
        nc.sync.dma_start(out=b_sb[:], in_=b.rearrange("(g p t) -> p g t", p=P, t=PACK))
        load_y(1, "y_raw1")
        load_y(2, "v_gpsimd")
        load_v(0, 0)
        load_c(1)
        load_y(3, "y_raw3")
        load_v(1, 0)
        load_c(2)
        load_x(1, 0)
        load_x(1, 1)
        load_v(2, 0)
        load_c(3)
        load_c(4)
        load_v(3, 0)
        load_c(5)
        load_c(6)
        load_c(7)
        load_v(2, 1)
        load_v(0, 1)
        load_v(3, 1)
        load_v(1, 1)

        y_codes, y_planes = {}, {}

        def sort_codes(g):
            y_codes[g] = keep([P, D_PASSES, PACK, P, 2], U8, "y_codes%d" % g)
            nc.vector.tensor_copy(
                out=y_codes[g][:],
                in_=y_raw[g][:].rearrange("p h (m t e) -> p h t m e", t=PACK, e=2))

        def sort_plane(g):
            staged = ys_raw[:, :, g * PASS:(g + 1) * PASS]
            y_planes[g] = keep([P, D_PASSES, PACK, P], U8, "y_planes%d" % g)
            nc.vector.tensor_copy(out=y_planes[g][:], in_=staged.rearrange("p h (m t) -> p h t m", t=PACK))

        def turn(bk, a, words):
            for u in range(2):
                col = (2 * a + u) * P
                nc.tensor.transpose(bk[:, col:col + P], words[:, u::2], ident[:])

        def join_words(dst, bk):
            nc.scalar.copy(out=dst.bitcast(F32).rearrange("p (a r u) -> p a r u", a=2, u=2),
                           in_=bk[:].rearrange("p (a u r) -> p a r u", a=2, u=2))

        x_banks, x_joined, x_mx = {}, {}, {}

        def turn_x(blk, pair, banks):
            for h in range(D_PASSES):
                x_banks[blk, pair, h] = bank(banks[h], "xt%d%d%d" % (blk, pair, h))
            for a in range(2):
                words = x_raw[blk, 2 * pair + a][:].bitcast(F32)
                for h in range(D_PASSES):
                    turn(x_banks[blk, pair, h], a, words[:, h * PAIR:(h + 1) * PAIR])

        def copy_x(blk, pair):
            for h in range(D_PASSES):
                x_joined[blk, pair, h] = rotate([P, PACK * PAIR], BF16, "x_joined%d%d%d" % (blk, pair, h),
                                                "x_joined", 2 * D_PASSES)
                join_words(x_joined[blk, pair, h][:], x_banks[blk, pair, h])

        def quantize_x(blk, pair):
            for h in range(D_PASSES):
                if pair == 0:
                    x_mx[blk, h] = mx_tiles("x%d%d" % (blk, h))
                codes, plane = x_mx[blk, h]
                cols = slice(pair * PAIR, (pair + 1) * PAIR)
                nc.vector.quantize_mx(out=codes[:, cols].bitcast(E4M3X4), scales=plane[:, cols],
                                      in_=x_joined[blk, pair, h][:])

        sim = {}

        def similarities(n, slots=range(PACK)):
            blk, g = divmod(n, N_PASSES)
            for t in slots:
                sim[n, t] = bank(SIM_BANKS[t], "sim%d_%d" % (n, t))
                for h in range(D_PASSES):
                    codes, plane = x_mx[blk, h]
                    nc.tensor.matmul_mx(
                        out=sim[n, t][:],
                        lhsT=y_codes[g][:, h, t, :, :].rearrange("p m e -> p (m e)").bitcast(E2M1X4),
                        lhsT_scale=y_planes[g][:, h, t, :],
                        rhs=codes[:].bitcast(E4M3X4), rhs_scale=plane[:],
                        start=(h == 0), stop=(h == D_PASSES - 1))

        c_banks, c_t, logit, sig, e_bf, e_mx = {}, {}, {}, {}, {}, {}

        def turn_c(n, banks):
            words = c_raw[n][:].bitcast(F32)
            for pair in range(2):
                c_banks[n, pair] = bank(banks[pair], "ct%d_%d" % (n, pair))
                for a in range(2):
                    turn(c_banks[n, pair], a, words[:, 2 * pair + a, :])

        def copy_c(n):
            c_t[n] = rotate([P, PACK * BANK], BF16, "c_t%d" % n, "c_t", C_BUFS)
            for pair in range(2):
                join_words(c_t[n][:, pair * PACK * PAIR:(pair + 1) * PACK * PAIR], c_banks[n, pair])

        def logits(n, lo=0, hi=BANK):
            g = n % N_PASSES
            c_slots = c_t[n][:].rearrange("p (i t) -> p t i", t=PACK)
            for u in range(2):
                logit[n, lo, u] = rotate([P, 2, hi - lo], F32, "logit%d_%d_%d" % (n, lo, u), "logit", LOGIT_BUFS)
                for e in range(2):
                    t = 2 * u + e
                    nc.vector.scalar_tensor_tensor(
                        out=logit[n, lo, u][:, e, :], in0=sim[n, t][:, lo:hi], scalar=b_sb[:, g, t:t + 1],
                        in1=c_slots[:, t, lo:hi], op0=ALU.add, op1=ALU.mult)

        def sigmoids(n, lo=0, hi=BANK, tag="sig"):
            tile = rotate([P, 2, hi - lo, 2], F32, "sig%d_%d" % (n, lo), tag, 2)
            sig.setdefault(n, []).append((lo, hi, tile))
            for u in range(2):
                nc.scalar.activation(out=tile[:, u, :, :], in_=logit[n, lo, u][:].rearrange("p e i -> p i e"),
                                     func=ACT.Sigmoid)

        def new_e(n, tag="e_bf"):
            e_bf[n] = rotate([P, PACK * BANK], BF16, "e_bf%d" % n, tag, 1)
            e_mx[n] = mx_tiles("e%d" % n)

        def make_e(n, lo, hi, engine=nc.vector):
            cols = slice(PACK * lo, PACK * hi)
            base, tile = [(s_lo, s) for s_lo, s_hi, s in sig[n] if s_lo <= lo and hi <= s_hi][0]
            engine.tensor_tensor(
                out=e_bf[n][:, cols].rearrange("p (i u e) -> p i u e", u=2, e=2),
                in0=tile[:, :, lo - base:hi - base, :].rearrange("p u i e -> p i u e"),
                in1=c_t[n][:, cols].rearrange("p (i u e) -> p i u e", u=2, e=2),
                op=ALU.mult)

        def quantize_e(n, lo=0, hi=BANK):
            codes, plane = e_mx[n]
            nc.vector.quantize_mx(out=codes[:, lo:hi].bitcast(E5M2X4), scales=plane[:, lo:hi],
                                  in_=e_bf[n][:, PACK * lo:PACK * hi])

        v_parts, v_mx = {}, {}

        def v_part(g, half, lo, hi, tag, bufs):
            tile = rotate([P, PACK * (hi - lo)], BF16, "v_part%d%d_%d" % (g, half, lo), tag, bufs)
            v_parts.setdefault((g, half), []).append((lo, hi, tile))
            return tile[:], v_raw[g, half][:, :, lo:hi]

        def interleave_v_scalar(g, half, lo, tag):
            dst, src = v_part(g, half, lo, BANK, tag, 2)
            nc.scalar.copy(out=dst.rearrange("p (d i t) -> p d t i", i=4, t=PACK),
                           in_=src.rearrange("p t (d i) -> p d t i", i=4))

        def v_whole_scalar(g, half):
            interleave_v_scalar(g, half, 0, "v_whole")

        def v_rest_scalar(g, half):
            interleave_v_scalar(g, half, GPSIMD_V_COLUMNS, "v_rest")

        def v_share_gpsimd(g, half):
            dst, src = v_part(g, half, 0, GPSIMD_V_COLUMNS, "v_gpsimd", 1)
            nc.gpsimd.tensor_scalar(out=dst.rearrange("p (d t) -> p d t", t=PACK), in0=src.rearrange("p t d -> p d t"),
                                    scalar1=1.0, scalar2=0.0, op0=ALU.mult, op1=ALU.add)

        def quantize_v(g, half):
            v_mx[g, half] = mx_tiles("v%d%d" % (g, half))
            codes, plane = v_mx[g, half]
            for lo, hi, tile in v_parts[g, half]:
                at = lo
                while at < hi:
                    width = max(w for w in (P, PAIR, BANK) if at + w <= hi)
                    nc.vector.quantize_mx(out=codes[:, at:at + width].bitcast(E4M3X4), scales=plane[:, at:at + width],
                                          in_=tile[:, PACK * (at - lo):PACK * (at - lo + width)])
                    at = at + width

        acc, passes_done = {}, {}

        def add_passes(blk, sums, gs):
            for g in gs:
                for a, half, k in sums:
                    done = passes_done.setdefault((blk, a, half), [])
                    done.append(g)
                    if len(done) == 1:
                        acc[blk, a, half] = bank(k, "acc%d%d%d" % (blk, a, half))
                    e_codes, e_plane = e_mx[blk * N_PASSES + g]
                    v_codes, v_plane = v_mx[g, half]
                    nc.tensor.matmul_mx(
                        out=acc[blk, a, half][:],
                        lhsT=e_codes[:, a * P:(a + 1) * P].bitcast(E5M2X4), lhsT_scale=e_plane[:, a * P:(a + 1) * P],
                        rhs=v_codes[:].bitcast(E4M3X4), rhs_scale=v_plane[:],
                        start=(len(done) == 1), stop=(len(done) == N_PASSES))

        def store(blk, a, half, copy=nc.scalar.copy):
            res = rotate([P, BANK], F32, "res%d%d%d" % (blk, a, half), "io", UNITS)
            copy(out=res[:], in_=acc[blk, a, half][:])
            row = blk * BANK + a * P
            nc.sync.dma_start(out=out[row:row + P, half * BANK:(half + 1) * BANK], in_=res[:])

        free_banks = LOW_BANKS + HIGH_BANKS
        left_sums = [(a, 0, free_banks[a]) for a in range(TILES)]
        right_sums = [(a, 1, free_banks[a]) for a in range(TILES)]
        last_banks = free_banks + SIM_BANKS
        tile_sums = [[(a, half, last_banks[2 * a + half]) for half in range(2)] for a in range(TILES)]

        turn_x(0, 0, LOW_BANKS)
        turn_x(0, 1, HIGH_BANKS)
        copy_x(0, 0)
        copy_x(0, 1)
        sort_codes(0)
        sort_plane(0)
        sort_plane(1)
        quantize_x(0, 0)
        sort_plane(2)
        sort_plane(3)
        quantize_x(0, 1)
        turn_c(0, LOW_BANKS)
        copy_c(0)
        similarities(0)
        sort_codes(1)
        sort_codes(2)
        v_rest_scalar(0, 0)
        turn_c(1, HIGH_BANKS)
        copy_c(1)

        v_share_gpsimd(0, 0)
        logits(0)
        similarities(1)
        sigmoids(0)
        sort_codes(3)
        quantize_v(0, 0)
        v_rest_scalar(1, 0)
        turn_c(2, LOW_BANKS)
        copy_c(2)

        v_share_gpsimd(1, 0)
        logits(1)
        turn_x(1, 0, HIGH_BANKS)
        similarities(2)
        sigmoids(1)
        new_e(0)
        make_e(0, 0, BANK)
        quantize_v(1, 0)
        quantize_e(0)
        copy_x(1, 0)
        turn_x(1, 1, LOW_BANKS)
        v_rest_scalar(2, 0)
        copy_x(1, 1)
        turn_c(3, HIGH_BANKS)

        v_share_gpsimd(2, 0)
        logits(2)
        similarities(3, (0, 1))
        turn_c(4, LOW_BANKS)
        similarities(3, (2, 3))
        copy_c(3)
        sigmoids(2)
        new_e(1)
        make_e(1, 0, BANK)
        quantize_x(1, 0)
        quantize_x(1, 1)
        quantize_v(2, 0)
        quantize_e(1)
        copy_c(4)
        turn_c(5, HIGH_BANKS)
        copy_c(5)
        v_rest_scalar(3, 0)

        v_share_gpsimd(3, 0)
        logits(3)
        turn_c(6, LOW_BANKS)
        similarities(4)
        copy_c(6)
        sigmoids(3)
        new_e(2)
        make_e(2, 0, BANK)
        quantize_v(3, 0)
        quantize_e(2)
        turn_c(7, HIGH_BANKS)
        v_rest_scalar(2, 1)
        copy_c(7)
        v_whole_scalar(0, 1)
        add_passes(0, left_sums, (0, 1))

        v_share_gpsimd(2, 1)
        logits(4)
        similarities(5)
        add_passes(0, left_sums, (2,))
        sigmoids(4)
        new_e(3)
        make_e(3, 0, BANK)
        quantize_v(0, 1)
        quantize_e(3)
        quantize_v(2, 1)
        add_passes(0, left_sums, (3,))
        v_rest_scalar(3, 1)
        v_whole_scalar(1, 1)

        v_share_gpsimd(3, 1)
        logits(5)
        for a in range(TILES):
            store(0, a, 0)
        similarities(6)
        quantize_v(3, 1)
        quantize_v(1, 1)
        for one_sum in right_sums:
            add_passes(0, [one_sum], (0, 2, 3, 1))
        sigmoids(5)
        for a in range(2):
            store(0, a, 1)
        new_e(4)
        make_e(4, 0, PAIR)
        make_e(4, PAIR, BANK)
        quantize_e(4, 0, PAIR)
        quantize_e(4, PAIR, BANK)

        new_e(5)
        make_e(5, 0, GPSIMD_E_IMAGES, nc.gpsimd)
        logits(6)
        similarities(7)
        sigmoids(6)
        for a in range(2, TILES):
            store(0, a, 1)
        make_e(5, GPSIMD_E_IMAGES, PAIR)
        make_e(5, PAIR, BANK)
        quantize_e(5, 0, PAIR)
        quantize_e(5, PAIR, BANK)
        for a in range(2):
            add_passes(1, tile_sums[a], (0, 1))

        new_e(6)
        new_e(7, "e_last")
        make_e(6, 0, GPSIMD_E_IMAGES, nc.gpsimd)
        logits(7, 0, PAIR)
        sigmoids(7, 0, PAIR)
        logits(7, PAIR, BANK)
        sigmoids(7, PAIR, BANK, "v_whole")
        add_passes(1, tile_sums[2] + tile_sums[3], (0, 1))
        for pair, first_image in ((0, GPSIMD_E_IMAGES), (1, PAIR)):
            lo, mid, hi = pair * PAIR, pair * PAIR + P, (pair + 1) * PAIR
            make_e(6, first_image, hi)
            make_e(7, lo, mid)
            quantize_e(6, lo, hi)
            make_e(7, mid, hi)
            quantize_e(7, lo, mid)
            quantize_e(7, mid, hi)
            for a in (2 * pair, 2 * pair + 1):
                add_passes(1, tile_sums[a], (2, 3))
        for a in range(TILES):
            store(1, a, 0)
            store(1, a, 1, nc.scalar.copy if a < 2 else nc.vector.tensor_copy)
